import numpy as np
import ml_dtypes


def mxq(x, axis, fmt="e4m3"):
    dtype, down = {"e4m3": (ml_dtypes.float8_e4m3fn, 7), "e5m2": (ml_dtypes.float8_e5m2, 14)}[fmt]
    v = np.moveaxis(np.asarray(x, np.float32).astype(ml_dtypes.bfloat16).astype(np.float64), axis, -1)
    blocks = v.reshape(v.shape[:-1] + (-1, 32))
    amax = np.abs(blocks).max(-1, keepdims=True)
    byte = np.maximum(np.where(amax > 0, np.frexp(amax)[1] - 1 + 127, 0) - down, 1)
    scale = np.exp2(byte - 127.0)
    codes = (blocks / scale).astype(np.float32).astype(dtype).astype(np.float64)
    return np.moveaxis((codes * scale).reshape(v.shape), -1, axis)


WIDE = False


def mx_kscale(k):
    if not WIDE:
        return np.ones(k)
    levels = np.array([10, -10, 5, -5, 0])
    if k % 512:
        return np.exp2(np.random.permutation(np.resize(levels, k // 32))).repeat(32)
    a = np.empty((k // 512, 16))
    for p in range(k // 512):
        a[p, :8] = np.random.permutation(np.resize(levels, 8))
        for g in range(8):
            far = levels[np.abs(levels - a[p, g]) >= 10]
            a[p, g + 8] = far[np.random.randint(len(far))]
    return np.exp2(a.ravel()).repeat(32)


def f64(x):
    return np.asarray(x).astype(np.float64)


def striped(idx):
    return np.tile(idx.reshape(-1, 16).T, (8, 1)).astype(np.uint16)


def unstriped(offs):
    return offs[:16].T.reshape(-1).astype(np.int64)


def pack_weight(w):
    k, n = w.shape
    w = f64(np.asarray(w, np.float32).astype(ml_dtypes.bfloat16)).reshape(k // 32, 32, n)
    amax = np.abs(w).max(1)
    byte = np.clip(np.where(amax > 0, np.frexp(amax)[1] - 1 + 127 - 7, 1), 1, 254)
    scaled = (w * np.exp2(127.0 - byte)[:, None, :]).reshape(k, n).astype(np.float32)
    words = np.ascontiguousarray(scaled.reshape(k // 512, 128, 4, n).transpose(0, 1, 3, 2)).astype(ml_dtypes.float8_e4m3fn).view(np.uint8)
    return words, np.ascontiguousarray(byte.astype(np.uint8).reshape(k // 512, 16, n))


def unpack_weight(words, scales):
    g, p, n, _ = words.shape
    vals = np.ascontiguousarray(words).view(ml_dtypes.float8_e4m3fn).astype(np.float64) * np.repeat(np.exp2(scales.astype(np.float64) - 127.0), 8, axis=1)[..., None]
    return vals.transpose(0, 1, 3, 2).reshape(g * 512, n)


def planes(y):
    n, m = y.shape
    v = y.astype(np.float32).astype(ml_dtypes.bfloat16).astype(np.float64).reshape(n // 32, 32, m)
    top = np.abs(v).max(1)
    byte = np.clip(np.where(top > 0, np.frexp(top)[1] - 1 + 127 - 7, 1), 1, 254)
    codes = (v * np.exp2(127.0 - byte)[:, None, :]).reshape(n, m).astype(np.float32).astype(ml_dtypes.float8_e4m3fn).view(np.uint8)
    words = codes.reshape(n // 512, 128, 4, m).transpose(0, 1, 3, 2)
    return np.ascontiguousarray(words), np.ascontiguousarray(byte.astype(np.uint8).reshape(n // 512, 16, m))


def sigmoid(v):
    return 1.0 / (1.0 + np.exp(-np.maximum(v, -700.0)))


def gelu(v):
    return 0.5 * v * (1.0 + np.tanh(np.sqrt(2.0 / np.pi) * (v + 0.044715 * v**3)))


K, T, S, H, N = 512, 1024, 512, 512, 512


def setup_inputs():
    n = np.random.standard_normal
    s = mx_kscale(K)[:, None]
    u = mx_kscale(H)
    packed_xT = pack_weight(n((K, T)) * s)
    packed_w1 = pack_weight(n((K, N)) / np.sqrt(2 * K) / s)
    packed_w2 = pack_weight(n((K, N)) / np.sqrt(2 * K) / s)
    packed_w5 = pack_weight(n((H, N)) / np.sqrt(H) / u[:, None])
    return {
        "x_words": packed_xT[0],
        "x_scales": packed_xT[1],
        "w1_words": packed_w1[0],
        "w1_scales": packed_w1[1],
        "w2_words": packed_w2[0],
        "w2_scales": packed_w2[1],
        "w3": (n((K, H)) / np.sqrt(2 * K) / s * u).astype(np.float32),
        "w4": (n((K, H)) / np.sqrt(2 * K) / s * u).astype(np.float32),
        "w5_words": packed_w5[0],
        "w5_scales": packed_w5[1],
        "offs": striped(np.random.permutation(T)[:S]),
        "prev": striped(np.random.permutation(T)[:S]),
    }


def reference(x_words, x_scales, w1_words, w1_scales, w2_words, w2_scales, w3, w4, w5_words, w5_scales, offs, prev):
    xq = unpack_weight(x_words, x_scales)[:, unstriped(offs)]
    x_prev = unpack_weight(x_words, x_scales)[:, unstriped(prev)]
    h = gelu(mxq(f64(w3), 0, "e4m3").T @ xq + mxq(f64(w4), 0, "e4m3").T @ x_prev)
    y = unpack_weight(w5_words, w5_scales).T @ mxq(h, 0, "e4m3")
    r = sigmoid(unpack_weight(w1_words, w1_scales).T @ xq + unpack_weight(w2_words, w2_scales).T @ x_prev)
    out_0 = y * r
    return (out_0,) + planes(out_0)

@@ -1,0 +1,215 @@
+from contextlib import ExitStack
+
+import concourse.mybir as mybir
+
+K, T, S, H, N = 512, 1024, 512, 512, 512
+FLOPS = 5 * 2 * 512 * 512 * 512
+
+F32 = mybir.dt.float32
+BF16 = mybir.dt.bfloat16
+I32 = mybir.dt.int32
+U32 = mybir.dt.uint32
+U16 = mybir.dt.uint16
+U8 = mybir.dt.uint8
+FP8X4 = mybir.dt.float8_e4m3fn_x4
+ACT = mybir.ActivationFunctionType
+ALU = mybir.AluOpType
+
+P = 128
+PACK = 4
+HALF = 256
+CHUNK = 128
+
+
+def tile_picked_zshift_gelu_po_kernel(
+    tc, x_words, x_scales, w1_words, w1_scales, w2_words, w2_scales, w3, w4, w5_words, w5_scales, offs, prev,
+    out_0, out_1, out_2,
+):
+    nc = tc.nc
+    with ExitStack() as ctx:
+        sb = ctx.enter_context(tc.tile_pool(name="sb", bufs=1))
+        psum = ctx.enter_context(tc.psum_pool(name="psum", bufs=4))
+
+        def tile(name, shape, dtype):
+            return sb.tile(shape, dtype, name=name, align_bytes=64)
+
+        def words_view(dram):
+            return dram[0].rearrange("p n t -> p (n t)").bitcast(I32)
+
+        def load_scale_rows(queue, plane, first, dram):
+            rows = dram[0].bitcast(I32)
+            for q in range(4):
+                queue.dma_start(plane[32 * q + first : 32 * q + first + 4, :].bitcast(I32), rows[4 * q : 4 * q + 4, :])
+
+        offs_sb = sb.tile([P, S // 16], U16, name="offs_sb")
+        prev_sb = sb.tile([P, S // 16], U16, name="prev_sb")
+        xw = tile("xw", [P, T], I32)
+        xs = tile("xs", [P, T], U8)
+        w12s_raw = tile("w12s_raw", [P, N], U8)
+        w5s_raw = tile("w5s_raw", [P, N], U8)
+        w1_raw = tile("w1_raw", [P, N], I32)
+        w2_raw = tile("w2_raw", [P, N], I32)
+        w5_raw = tile("w5_raw", [P, N], I32)
+        w3_raw = [tile(f"w3_raw{u}", [P, PACK, HALF], F32) for u in range(2)]
+        w4_raw = tile("w4_raw", [P, PACK, H], F32)
+
+        w3_rows = w3.rearrange("(p j) c -> p j c", j=PACK)
+        nc.gpsimd.memset(w12s_raw[:].bitcast(I32), 0)
+        nc.sync.dma_start(offs_sb[:], offs)
+        nc.sync.dma_start(xw[:], words_view(x_words))
+        nc.vector.memset(xs[:].bitcast(I32), 0)
+        load_scale_rows(nc.scalar, xs, 0, x_scales)
+        nc.vector.memset(w5s_raw[:].bitcast(I32), 0)
+        nc.sync.dma_start(prev_sb[:], prev)
+        nc.sync.dma_start(w3_raw[0][:], w3_rows[:, :, 0:HALF])
+        load_scale_rows(nc.gpsimd, w12s_raw, 0, w1_scales)
+        nc.sync.dma_start(w3_raw[1][:], w3_rows[:, :, HALF:H])
+        nc.sync.dma_start(w1_raw[:], words_view(w1_words))
+        load_scale_rows(nc.sync, w12s_raw, 4, w2_scales)
+        nc.sync.dma_start(w2_raw[:], words_view(w2_words))
+        nc.sync.dma_start(w4_raw[:], w4.rearrange("(p j) c -> p j c", j=PACK))
+        nc.sync.dma_start(w5_raw[:], words_view(w5_words))
+        load_scale_rows(nc.sync, w5s_raw, 0, w5_scales)
+
+        xq_w = [tile(f"xq_w{u}", [P, HALF], I32) for u in range(2)]
+        xp_w = [tile(f"xp_w{u}", [P, HALF], I32) for u in range(2)]
+        xq_s = [tile(f"xq_s{u}", [P, HALF], U8) for u in range(2)]
+        xp_s = [tile(f"xp_s{u}", [P, HALF], U8) for u in range(2)]
+
+        def gather(u):
+            cols = slice(u * HALF // 16, (u + 1) * HALF // 16)
+            nc.vector.tensor_copy(xq_w[u][:].bitcast(U32), xw[:].bitcast(U32).indirect(offs_sb[:, cols]))
+            nc.vector.tensor_copy(xp_w[u][:].bitcast(U32), xw[:].bitcast(U32).indirect(prev_sb[:, cols]))
+            nc.vector.tensor_copy(xq_s[u][:], xs[:].indirect(offs_sb[:, cols]))
+            nc.vector.tensor_copy(xp_s[u][:], xs[:].indirect(prev_sb[:, cols]))
+
+        def deal_words(name, raw):
+            dealt = tile(name, [P, N], I32)
+            nc.vector.tensor_copy(
+                dealt[:].rearrange("p (t c i) -> p c t i", t=PACK, i=4),
+                raw[:].rearrange("p (c i t) -> p c t i", t=PACK, i=4),
+            )
+            return dealt
+
+        def deal_scales(name, raw):
+            dealt = tile(name, [P, N], U8)
+            nc.vector.tensor_copy(
+                dealt[:].rearrange("p (t c i) -> p c t i", t=PACK, i=16),
+                raw[:].rearrange("p (c i t) -> p c t i", t=PACK, i=16),
+            )
+            return dealt
+
+        def cast(copy, grouped, m0, raw):
+            ms = raw.shape[2] // PACK
+            copy(
+                grouped[:, :, m0 : m0 + ms, :].rearrange("p t m j -> p m t j"),
+                raw.rearrange("p j (m t) -> p m t j", t=PACK),
+            )
+
+        def quantize(name, grouped, width):
+            codes = tile(name + "_w", [P, width], I32)
+            plane = tile(name + "_s", [P, width], U8)
+            nc.vector.quantize_mx(out=codes[:].bitcast(FP8X4), scales=plane[:], in_=grouped)
+            return codes, plane
+
+        def mm(out, lw, ls, rw, rs, start, stop):
+            nc.tensor.matmul_mx(out=out, lhsT=lw.bitcast(FP8X4), lhsT_scale=ls, rhs=rw.bitcast(FP8X4), rhs_scale=rs, start=start, stop=stop)
+
+        w3_g = tile("w3_g", [P, PACK, P, PACK], BF16)
+        w4_g = tile("w4_g", [P, PACK, P, PACK], BF16)
+        gate = [tile(f"gate{u}", [P, PACK, HALF], F32) for u in range(2)]
+
+        def gate_products(u):
+            for pair in range(2):
+                bank = psum.tile([P, 2, HALF], F32, name="ry")
+                for e in range(2):
+                    cols = slice((2 * pair + e) * P, (2 * pair + e + 1) * P)
+                    mm(bank[:, e, :], w1d[:, cols], w12s[:, cols], xq_w[u][:], xq_s[u][:], True, False)
+                    mm(bank[:, e, :], w2d[:, cols], w12s[4:, cols], xp_w[u][:], xp_s[u][:], False, True)
+                nc.scalar.activation(gate[u][:, 2 * pair : 2 * pair + 2, :], bank[:], ACT.Tanh, scale=0.5)
+
+        def gate_affine(u):
+            nc.vector.tensor_scalar(gate[u][:], gate[u][:], 0.5, 0.5, ALU.mult, ALU.add)
+
+        def hidden(c):
+            u, tok = c // 2, slice((c % 2) * CHUNK, (c % 2 + 1) * CHUNK)
+            bank = psum.tile([P, PACK, CHUNK], F32, name="hb")
+            for t in range(PACK):
+                cols = slice(t * P, (t + 1) * P)
+                mm(bank[:, t, :], w3q[0][:, cols], w3q[1][:, cols], xq_w[u][:, tok], xq_s[u][:, tok], True, False)
+                mm(bank[:, t, :], w4q[0][:, cols], w4q[1][:, cols], xp_w[u][:, tok], xp_s[u][:, tok], False, True)
+            h_g = tile(f"h_g{c}", [P, CHUNK, PACK], BF16)
+            nc.scalar.activation(h_g[:], bank[:].rearrange("p t n -> p n t"), ACT.Gelu_apprx_tanh)
+            return h_g
+
+        def second(c, h_g):
+            hw, hs = quantize(f"h{c}", h_g[:].rearrange("p n t -> p (n t)"), CHUNK)
+            bank = psum.tile([P, PACK, CHUNK], F32, name="ry")
+            for t in range(PACK):
+                cols = slice(t * P, (t + 1) * P)
+                mm(bank[:, t, :], w5d[:, cols], w5s[:, cols], hw[:], hs[:], True, True)
+            return bank
+
+        out_rows = out_0.rearrange("(p t) n -> p t n", t=PACK)
+        o_w = [tile(f"o_w{u}", [P, HALF], I32) for u in range(2)]
+        o_s = tile("o_s", [P, S], U8)
+
+        def gated(c, bank):
+            u, tok = c // 2, slice((c % 2) * CHUNK, (c % 2 + 1) * CHUNK)
+            res = tile(f"res{c}", [P, PACK, CHUNK], F32)
+            nc.vector.tensor_tensor(res[:], bank[:], gate[u][:, :, tok], ALU.mult)
+            nc.sync.dma_start(out_rows[:, :, c * CHUNK : (c + 1) * CHUNK], res[:])
+            return res
+
+        def regroup(c, res, copy):
+            o_g = tile(f"o_g{c}", [P, CHUNK, PACK], BF16)
+            copy(o_g[:].rearrange("p (c i) t -> p c t i", i=4), res[:].rearrange("p t (c i) -> p c t i", i=4))
+            return o_g
+
+        def planes(c, o_g):
+            u, tok = c // 2, slice((c % 2) * CHUNK, (c % 2 + 1) * CHUNK)
+            nc.vector.quantize_mx(
+                out=o_w[u][:, tok].bitcast(FP8X4),
+                scales=o_s[:, c * CHUNK : (c + 1) * CHUNK],
+                in_=o_g[:].rearrange("p n t -> p (n t)"),
+            )
+            if c % 2 == 1:
+                nc.sync.dma_start(words_view(out_1)[:, u * HALF : (u + 1) * HALF], o_w[u][:])
+
+        cast(nc.scalar.copy, w3_g, 0, w3_raw[0][:])
+        gather(0)
+        cast(nc.scalar.copy, w3_g, 64, w3_raw[1][:])
+        w1d = deal_words("w1d", w1_raw)
+        w2d = deal_words("w2d", w2_raw)
+        w12s = deal_scales("w12s", w12s_raw)
+        gate_products(0)
+        gather(1)
+        w3q = quantize("w3q", w3_g[:].rearrange("p t m j -> p (t m j)"), H)
+        cast(nc.scalar.copy, w4_g, 0, w4_raw[:, :, 0:HALF])
+        cast(nc.vector.tensor_copy, w4_g, 64, w4_raw[:, :, HALF:H])
+        gate_products(1)
+        w4q = quantize("w4q", w4_g[:].rearrange("p t m j -> p (t m j)"), H)
+        h_gs = [hidden(c) for c in range(4)]
+        w5d = deal_words("w5d", w5_raw)
+        w5s = deal_scales("w5s", w5s_raw)
+        gate_affine(0)
+        banks = [second(0, h_gs[0])]
+        gate_affine(1)
+        banks.append(second(1, h_gs[1]))
+        res = [gated(0, banks[0])]
+        banks.append(second(2, h_gs[2]))
+        res.append(gated(1, banks[1]))
+        banks.append(second(3, h_gs[3]))
+        o_gs = [regroup(0, res[0], nc.scalar.copy), regroup(1, res[1], nc.scalar.copy)]
+        res.append(gated(2, banks[2]))
+        planes(0, o_gs[0])
+        o_gs.append(regroup(2, res[2], nc.scalar.copy))
+        res.append(gated(3, banks[3]))
+        planes(1, o_gs[1])
+        o_gs.append(regroup(3, res[3], nc.scalar.copy))
+        planes(2, o_gs[2])
+        planes(3, o_gs[3])
+        scale_rows = out_2[0].bitcast(I32)
+        for q in range(4):
+            queue = nc.sync if q % 2 == 0 else nc.scalar
+            queue.dma_start(scale_rows[4 * q : 4 * q + 4, :], o_s[32 * q : 32 * q + 4, :].bitcast(I32))

@@ -28,71 +28,72 @@ def tile_picked_zshift_gelu_po_kernel(
     nc = tc.nc
     with ExitStack() as ctx:
         sb = ctx.enter_context(tc.tile_pool(name="sb", bufs=1))
-        psum = ctx.enter_context(tc.psum_pool(name="psum", bufs=4))
+        psum = ctx.enter_context(tc.psum_pool(name="psum", bufs=1))
 
-        def tile(name, shape, dtype):
-            return sb.tile(shape, dtype, name=name, align_bytes=64)
+        def tile(name, shape, dtype, tag=None):
+            return sb.tile(shape, dtype, name=name, tag=tag or name, align_bytes=64)
 
         def words_view(dram):
             return dram[0].rearrange("p n t -> p (n t)").bitcast(I32)
 
-        def load_scale_rows(queue, plane, first, dram):
+        def load_scale_rows(queue, first, dram, quadrants):
             rows = dram[0].bitcast(I32)
-            for q in range(4):
-                queue.dma_start(plane[32 * q + first : 32 * q + first + 4, :].bitcast(I32), rows[4 * q : 4 * q + 4, :])
+            for q in quadrants:
+                queue.dma_start(ws_raw[32 * q + first : 32 * q + first + 4, :].bitcast(I32), rows[4 * q : 4 * q + 4, :])
 
         offs_sb = sb.tile([P, S // 16], U16, name="offs_sb")
         prev_sb = sb.tile([P, S // 16], U16, name="prev_sb")
         xw = tile("xw", [P, T], I32)
         xs = tile("xs", [P, T], U8)
-        w12s_raw = tile("w12s_raw", [P, N], U8)
-        w5s_raw = tile("w5s_raw", [P, N], U8)
+        ws_raw = tile("ws_raw", [P, N], U8)
         w1_raw = tile("w1_raw", [P, N], I32)
         w2_raw = tile("w2_raw", [P, N], I32)
         w5_raw = tile("w5_raw", [P, N], I32)
-        w3_raw = [tile(f"w3_raw{u}", [P, PACK, HALF], F32) for u in range(2)]
+        w3_raw = tile("w3_raw", [P, PACK, H], F32)
         w4_raw = tile("w4_raw", [P, PACK, H], F32)
 
-        w3_rows = w3.rearrange("(p j) c -> p j c", j=PACK)
-        nc.gpsimd.memset(w12s_raw[:].bitcast(I32), 0)
-        nc.sync.dma_start(offs_sb[:], offs)
+        warm = tile("warm", [P, 2], F32)
+        nc.vector.memset(ws_raw[:].bitcast(I32), 0)
+        nc.vector.memset(warm[:, 0:1], 0.0)
+        nc.scalar.activation(warm[:, 1:2], warm[:, 0:1], ACT.Gelu_apprx_tanh)
         nc.sync.dma_start(xw[:], words_view(x_words))
-        nc.vector.memset(xs[:].bitcast(I32), 0)
-        load_scale_rows(nc.scalar, xs, 0, x_scales)
-        nc.vector.memset(w5s_raw[:].bitcast(I32), 0)
+        nc.sync.dma_start(offs_sb[:], offs)
         nc.sync.dma_start(prev_sb[:], prev)
-        nc.sync.dma_start(w3_raw[0][:], w3_rows[:, :, 0:HALF])
-        load_scale_rows(nc.gpsimd, w12s_raw, 0, w1_scales)
-        nc.sync.dma_start(w3_raw[1][:], w3_rows[:, :, HALF:H])
-        nc.sync.dma_start(w1_raw[:], words_view(w1_words))
-        load_scale_rows(nc.sync, w12s_raw, 4, w2_scales)
-        nc.sync.dma_start(w2_raw[:], words_view(w2_words))
+        x_rows = x_scales[0].bitcast(I32)
+        for q in range(4):
+            nc.sync.dma_start(xs[32 * q : 32 * q + 32, :].bitcast(I32), x_rows[4 * q : 4 * q + 4, :].unsqueeze(0).to_broadcast([8, 4, T // 4]))
+        nc.sync.dma_start(w3_raw[:], w3.rearrange("(p j) c -> p j c", j=PACK))
+        load_scale_rows(nc.sync, 0, w1_scales, range(2))
         nc.sync.dma_start(w4_raw[:], w4.rearrange("(p j) c -> p j c", j=PACK))
+        load_scale_rows(nc.sync, 0, w1_scales, range(2, 4))
+        load_scale_rows(nc.sync, 4, w2_scales, range(2))
+        nc.sync.dma_start(w1_raw[:], words_view(w1_words))
+        load_scale_rows(nc.sync, 4, w2_scales, range(2, 4))
+        nc.sync.dma_start(w2_raw[:], words_view(w2_words))
+        load_scale_rows(nc.sync, 8, w5_scales, range(4))
         nc.sync.dma_start(w5_raw[:], words_view(w5_words))
-        load_scale_rows(nc.sync, w5s_raw, 0, w5_scales)
 
-        xq_w = [tile(f"xq_w{u}", [P, HALF], I32) for u in range(2)]
-        xp_w = [tile(f"xp_w{u}", [P, HALF], I32) for u in range(2)]
-        xq_s = [tile(f"xq_s{u}", [P, HALF], U8) for u in range(2)]
-        xp_s = [tile(f"xp_s{u}", [P, HALF], U8) for u in range(2)]
+        xq_w = tile("xq_w", [P, S], I32)
+        xp_w = tile("xp_w", [P, S], I32)
+        xq_s = tile("xq_s", [P, S], U8)
+        xp_s = tile("xp_s", [P, S], U8)
 
-        def gather(u):
-            cols = slice(u * HALF // 16, (u + 1) * HALF // 16)
-            nc.vector.tensor_copy(xq_w[u][:].bitcast(U32), xw[:].bitcast(U32).indirect(offs_sb[:, cols]))
-            nc.vector.tensor_copy(xp_w[u][:].bitcast(U32), xw[:].bitcast(U32).indirect(prev_sb[:, cols]))
-            nc.vector.tensor_copy(xq_s[u][:], xs[:].indirect(offs_sb[:, cols]))
-            nc.vector.tensor_copy(xp_s[u][:], xs[:].indirect(prev_sb[:, cols]))
+        def gather():
+            nc.vector.tensor_copy(xq_w[:].bitcast(U32), xw[:].bitcast(U32).indirect(offs_sb[:]))
+            nc.vector.tensor_copy(xp_w[:].bitcast(U32), xw[:].bitcast(U32).indirect(prev_sb[:]))
+            nc.vector.tensor_copy(xq_s[:], xs[:].indirect(offs_sb[:]))
+            nc.vector.tensor_copy(xp_s[:], xs[:].indirect(prev_sb[:]))
 
-        def deal_words(name, raw):
-            dealt = tile(name, [P, N], I32)
+        def deal_words(name, raw, tag=None):
+            dealt = tile(name, [P, N], I32, tag)
             nc.vector.tensor_copy(
                 dealt[:].rearrange("p (t c i) -> p c t i", t=PACK, i=4),
                 raw[:].rearrange("p (c i t) -> p c t i", t=PACK, i=4),
             )
             return dealt
 
-        def deal_scales(name, raw):
-            dealt = tile(name, [P, N], U8)
+        def deal_scales(name, raw, tag=None):
+            dealt = tile(name, [P, N], U8, tag)
             nc.vector.tensor_copy(
                 dealt[:].rearrange("p (t c i) -> p c t i", t=PACK, i=16),
                 raw[:].rearrange("p (c i t) -> p c t i", t=PACK, i=16),
@@ -106,9 +107,9 @@ def tile_picked_zshift_gelu_po_kernel(
                 raw.rearrange("p j (m t) -> p m t j", t=PACK),
             )
 
-        def quantize(name, grouped, width):
-            codes = tile(name + "_w", [P, width], I32)
-            plane = tile(name + "_s", [P, width], U8)
+        def quantize(name, grouped, width, tags=(None, None)):
+            codes = tile(name + "_w", [P, width], I32, tags[0])
+            plane = tile(name + "_s", [P, width], U8, tags[1])
             nc.vector.quantize_mx(out=codes[:].bitcast(FP8X4), scales=plane[:], in_=grouped)
             return codes, plane
 
@@ -117,53 +118,62 @@ def tile_picked_zshift_gelu_po_kernel(
 
         w3_g = tile("w3_g", [P, PACK, P, PACK], BF16)
         w4_g = tile("w4_g", [P, PACK, P, PACK], BF16)
-        gate = [tile(f"gate{u}", [P, PACK, HALF], F32) for u in range(2)]
+        gate = []
+
+        banks = [psum.tile([P, PACK, CHUNK], F32, name=f"bank{b}") for b in range(6)]
+        hy_bank = banks[0:4]
+        gate_bank = banks[2:6]
 
         def gate_products(u):
+            tok = slice(u * HALF, (u + 1) * HALF)
+            gate.append(tile(f"gate{u}", [P, PACK, HALF], F32))
             for pair in range(2):
-                bank = psum.tile([P, 2, HALF], F32, name="ry")
+                bank = gate_bank[2 * u + pair][:].rearrange("p (e a) n -> p e (a n)", e=2)
                 for e in range(2):
                     cols = slice((2 * pair + e) * P, (2 * pair + e + 1) * P)
-                    mm(bank[:, e, :], w1d[:, cols], w12s[:, cols], xq_w[u][:], xq_s[u][:], True, False)
-                    mm(bank[:, e, :], w2d[:, cols], w12s[4:, cols], xp_w[u][:], xp_s[u][:], False, True)
-                nc.scalar.activation(gate[u][:, 2 * pair : 2 * pair + 2, :], bank[:], ACT.Tanh, scale=0.5)
+                    mm(bank[:, e, :], w1d[:, cols], ws[:, cols], xq_w[:, tok], xq_s[:, tok], True, False)
+                    mm(bank[:, e, :], w2d[:, cols], ws[4:, cols], xp_w[:, tok], xp_s[:, tok], False, True)
+                nc.scalar.activation(gate[u][:, 2 * pair : 2 * pair + 2, :], bank, ACT.Tanh, scale=0.5)
 
         def gate_affine(u):
             nc.vector.tensor_scalar(gate[u][:], gate[u][:], 0.5, 0.5, ALU.mult, ALU.add)
 
         def hidden(c):
-            u, tok = c // 2, slice((c % 2) * CHUNK, (c % 2 + 1) * CHUNK)
-            bank = psum.tile([P, PACK, CHUNK], F32, name="hb")
+            tok = slice(c * CHUNK, (c + 1) * CHUNK)
+            bank = hy_bank[c]
             for t in range(PACK):
                 cols = slice(t * P, (t + 1) * P)
-                mm(bank[:, t, :], w3q[0][:, cols], w3q[1][:, cols], xq_w[u][:, tok], xq_s[u][:, tok], True, False)
-                mm(bank[:, t, :], w4q[0][:, cols], w4q[1][:, cols], xp_w[u][:, tok], xp_s[u][:, tok], False, True)
+                mm(bank[:, t, :], w3q[0][:, cols], w3q[1][:, cols], xq_w[:, tok], xq_s[:, tok], True, False)
+                mm(bank[:, t, :], w4q[0][:, cols], w4q[1][:, cols], xp_w[:, tok], xp_s[:, tok], False, True)
             h_g = tile(f"h_g{c}", [P, CHUNK, PACK], BF16)
             nc.scalar.activation(h_g[:], bank[:].rearrange("p t n -> p n t"), ACT.Gelu_apprx_tanh)
-            return h_g
+            h_gs.append(h_g)
 
-        def second(c, h_g):
-            hw, hs = quantize(f"h{c}", h_g[:].rearrange("p n t -> p (n t)"), CHUNK)
-            bank = psum.tile([P, PACK, CHUNK], F32, name="ry")
+        def hidden_codes(c):
+            tok = slice(c * CHUNK, (c + 1) * CHUNK)
+            nc.vector.quantize_mx(out=h_w[:, tok].bitcast(FP8X4), scales=h_s[:, tok], in_=h_gs[c][:].rearrange("p n t -> p (n t)"))
+
+        def second(c):
+            tok = slice(c * CHUNK, (c + 1) * CHUNK)
+            bank = hy_bank[c]
             for t in range(PACK):
                 cols = slice(t * P, (t + 1) * P)
-                mm(bank[:, t, :], w5d[:, cols], w5s[:, cols], hw[:], hs[:], True, True)
-            return bank
+                mm(bank[:, t, :], w5d[:, cols], ws[8:, cols], h_w[:, tok], h_s[:, tok], True, True)
 
         out_rows = out_0.rearrange("(p t) n -> p t n", t=PACK)
         o_w = [tile(f"o_w{u}", [P, HALF], I32) for u in range(2)]
         o_s = tile("o_s", [P, S], U8)
 
-        def gated(c, bank):
+        def gated(c):
             u, tok = c // 2, slice((c % 2) * CHUNK, (c % 2 + 1) * CHUNK)
             res = tile(f"res{c}", [P, PACK, CHUNK], F32)
-            nc.vector.tensor_tensor(res[:], bank[:], gate[u][:, :, tok], ALU.mult)
+            nc.vector.tensor_tensor(res[:], hy_bank[c][:], gate[u][:, :, tok], ALU.mult)
             nc.sync.dma_start(out_rows[:, :, c * CHUNK : (c + 1) * CHUNK], res[:])
             return res
 
         def regroup(c, res, copy):
             o_g = tile(f"o_g{c}", [P, CHUNK, PACK], BF16)
-            copy(o_g[:].rearrange("p (c i) t -> p c t i", i=4), res[:].rearrange("p t (c i) -> p c t i", i=4))
+            copy(o_g[:], res[:].rearrange("p t n -> p n t"))
             return o_g
 
         def planes(c, o_g):
@@ -176,37 +186,37 @@ def tile_picked_zshift_gelu_po_kernel(
             if c % 2 == 1:
                 nc.sync.dma_start(words_view(out_1)[:, u * HALF : (u + 1) * HALF], o_w[u][:])
 
-        cast(nc.scalar.copy, w3_g, 0, w3_raw[0][:])
-        gather(0)
-        cast(nc.scalar.copy, w3_g, 64, w3_raw[1][:])
-        w1d = deal_words("w1d", w1_raw)
-        w2d = deal_words("w2d", w2_raw)
-        w12s = deal_scales("w12s", w12s_raw)
-        gate_products(0)
-        gather(1)
-        w3q = quantize("w3q", w3_g[:].rearrange("p t m j -> p (t m j)"), H)
+        cast(nc.scalar.copy, w3_g, 0, w3_raw[:])
+        gather()
         cast(nc.scalar.copy, w4_g, 0, w4_raw[:, :, 0:HALF])
         cast(nc.vector.tensor_copy, w4_g, 64, w4_raw[:, :, HALF:H])
-        gate_products(1)
+        w3q = quantize("w3q", w3_g[:].rearrange("p t m j -> p (t m j)"), H)
         w4q = quantize("w4q", w4_g[:].rearrange("p t m j -> p (t m j)"), H)
-        h_gs = [hidden(c) for c in range(4)]
-        w5d = deal_words("w5d", w5_raw)
-        w5s = deal_scales("w5s", w5s_raw)
+        h_gs, res, o_gs = [], [], []
+        hidden(0)
+        hidden(1)
+        w1d = deal_words("w1d", w1_raw, "w4_g")
+        w2d = deal_words("w2d", w2_raw, "w1_raw")
+        ws = deal_scales("ws", ws_raw, "w2_raw")
+        w5d = deal_words("w5d", w5_raw, "ws_raw")
+        h_w = tile("h_w", [P, S], I32)
+        h_s = tile("h_s", [P, S], U8, "w5_raw")
+        hidden_codes(0)
+        hidden_codes(1)
+        gate_products(0)
+        gate_products(1)
         gate_affine(0)
-        banks = [second(0, h_gs[0])]
         gate_affine(1)
-        banks.append(second(1, h_gs[1]))
-        res = [gated(0, banks[0])]
-        banks.append(second(2, h_gs[2]))
-        res.append(gated(1, banks[1]))
-        banks.append(second(3, h_gs[3]))
-        o_gs = [regroup(0, res[0], nc.scalar.copy), regroup(1, res[1], nc.scalar.copy)]
-        res.append(gated(2, banks[2]))
-        planes(0, o_gs[0])
-        o_gs.append(regroup(2, res[2], nc.scalar.copy))
-        res.append(gated(3, banks[3]))
-        planes(1, o_gs[1])
-        o_gs.append(regroup(3, res[3], nc.scalar.copy))
+        for c in range(2):
+            hidden(c + 2)
+            second(c)
+            hidden_codes(c + 2)
+        for c in range(4):
+            if c >= 2:
+                second(c)
+                planes(c - 2, o_gs[c - 2])
+            res.append(gated(c))
+            o_gs.append(regroup(c, res[c], nc.scalar.copy if c < 3 else nc.vector.tensor_copy))
         planes(2, o_gs[2])
         planes(3, o_gs[3])
         scale_rows = out_2[0].bitcast(I32)

@@ -53,6 +53,7 @@ def tile_picked_zshift_gelu_po_kernel(
         w4_raw = tile("w4_raw", [P, PACK, H], F32)
 
         warm = tile("warm", [P, 2], F32)
+        nc.vector.memset(xs[:].bitcast(I32), 0)
         nc.vector.memset(ws_raw[:].bitcast(I32), 0)
         nc.vector.memset(warm[:, 0:1], 0.0)
         nc.scalar.activation(warm[:, 1:2], warm[:, 0:1], ACT.Gelu_apprx_tanh)
@@ -61,7 +62,7 @@ def tile_picked_zshift_gelu_po_kernel(
         nc.sync.dma_start(prev_sb[:], prev)
         x_rows = x_scales[0].bitcast(I32)
         for q in range(4):
-            nc.sync.dma_start(xs[32 * q : 32 * q + 32, :].bitcast(I32), x_rows[4 * q : 4 * q + 4, :].unsqueeze(0).to_broadcast([8, 4, T // 4]))
+            nc.sync.dma_start(xs[32 * q : 32 * q + 4, :].bitcast(I32), x_rows[4 * q : 4 * q + 4, :])
         nc.sync.dma_start(w3_raw[:], w3.rearrange("(p j) c -> p j c", j=PACK))
         load_scale_rows(nc.sync, 0, w1_scales, range(2))
         nc.sync.dma_start(w4_raw[:], w4.rearrange("(p j) c -> p j c", j=PACK))
@@ -161,38 +162,36 @@ def tile_picked_zshift_gelu_po_kernel(
                 mm(bank[:, t, :], w5d[:, cols], ws[8:, cols], h_w[:, tok], h_s[:, tok], True, True)
 
         out_rows = out_0.rearrange("(p t) n -> p t n", t=PACK)
-        o_w = [tile(f"o_w{u}", [P, HALF], I32) for u in range(2)]
+        o_w = tile("o_w", [P, S], I32)
         o_s = tile("o_s", [P, S], U8)
+        pieces = [slice(0, 256), slice(256, 384), slice(384, 512)]
+        res = [tile(f"res{i}", [P, PACK, s.stop - s.start], F32) for i, s in enumerate(pieces)]
+        o_g = [tile(f"o_g{i}", [P, s.stop - s.start, PACK], BF16) for i, s in enumerate(pieces)]
 
         def gated(c):
             u, tok = c // 2, slice((c % 2) * CHUNK, (c % 2 + 1) * CHUNK)
-            res = tile(f"res{c}", [P, PACK, CHUNK], F32)
-            nc.vector.tensor_tensor(res[:], hy_bank[c][:], gate[u][:, :, tok], ALU.mult)
-            nc.sync.dma_start(out_rows[:, :, c * CHUNK : (c + 1) * CHUNK], res[:])
-            return res
+            dst = res[0][:, :, tok] if c < 2 else res[c - 1][:]
+            nc.vector.tensor_tensor(dst, hy_bank[c][:], gate[u][:, :, tok], ALU.mult)
 
-        def regroup(c, res, copy):
-            o_g = tile(f"o_g{c}", [P, CHUNK, PACK], BF16)
-            copy(o_g[:], res[:].rearrange("p t n -> p n t"))
-            return o_g
+        def hand_out(i, copy):
+            nc.sync.dma_start(out_rows[:, :, pieces[i]], res[i][:])
+            copy(o_g[i][:], res[i][:].rearrange("p t n -> p n t"))
 
-        def planes(c, o_g):
-            u, tok = c // 2, slice((c % 2) * CHUNK, (c % 2 + 1) * CHUNK)
+        def planes(i):
             nc.vector.quantize_mx(
-                out=o_w[u][:, tok].bitcast(FP8X4),
-                scales=o_s[:, c * CHUNK : (c + 1) * CHUNK],
-                in_=o_g[:].rearrange("p n t -> p (n t)"),
+                out=o_w[:, pieces[i]].bitcast(FP8X4),
+                scales=o_s[:, pieces[i]],
+                in_=o_g[i][:].rearrange("p n t -> p (n t)"),
             )
-            if c % 2 == 1:
-                nc.sync.dma_start(words_view(out_1)[:, u * HALF : (u + 1) * HALF], o_w[u][:])
 
-        cast(nc.scalar.copy, w3_g, 0, w3_raw[:])
+        cast(nc.scalar.copy, w3_g, 0, w3_raw[:, :, 0:384])
         gather()
-        cast(nc.scalar.copy, w4_g, 0, w4_raw[:, :, 0:HALF])
-        cast(nc.vector.tensor_copy, w4_g, 64, w4_raw[:, :, HALF:H])
-        w3q = quantize("w3q", w3_g[:].rearrange("p t m j -> p (t m j)"), H)
+        cast(nc.vector.tensor_copy, w3_g, 96, w3_raw[:, :, 384:H])
+        cast(nc.scalar.copy, w4_g, 0, w4_raw[:, :, 0:128])
+        cast(nc.vector.tensor_copy, w4_g, 32, w4_raw[:, :, 128:H])
+        w3q = quantize("w3q", w3_g[:].rearrange("p t m j -> p (t m j)"), H, ("w4_raw", None))
         w4q = quantize("w4q", w4_g[:].rearrange("p t m j -> p (t m j)"), H)
-        h_gs, res, o_gs = [], [], []
+        h_gs = []
         hidden(0)
         hidden(1)
         w1d = deal_words("w1d", w1_raw, "w4_g")
@@ -211,14 +210,19 @@ def tile_picked_zshift_gelu_po_kernel(
             hidden(c + 2)
             second(c)
             hidden_codes(c + 2)
-        for c in range(4):
-            if c >= 2:
-                second(c)
-                planes(c - 2, o_gs[c - 2])
-            res.append(gated(c))
-            o_gs.append(regroup(c, res[c], nc.scalar.copy if c < 3 else nc.vector.tensor_copy))
-        planes(2, o_gs[2])
-        planes(3, o_gs[3])
+        gated(0)
+        gated(1)
+        hand_out(0, nc.scalar.copy)
+        second(2)
+        gated(2)
+        hand_out(1, nc.scalar.copy)
+        second(3)
+        gated(3)
+        planes(0)
+        hand_out(2, nc.vector.tensor_copy)
+        planes(1)
+        planes(2)
+        nc.scalar.dma_start(words_view(out_1), o_w[:])
         scale_rows = out_2[0].bitcast(I32)
         for q in range(4):
             queue = nc.sync if q % 2 == 0 else nc.scalar

@@ -64,13 +64,12 @@ def tile_picked_zshift_gelu_po_kernel(
         for q in range(4):
             nc.sync.dma_start(xs[32 * q : 32 * q + 4, :].bitcast(I32), x_rows[4 * q : 4 * q + 4, :])
         nc.sync.dma_start(w3_raw[:], w3.rearrange("(p j) c -> p j c", j=PACK))
-        load_scale_rows(nc.sync, 0, w1_scales, range(2))
         nc.sync.dma_start(w4_raw[:], w4.rearrange("(p j) c -> p j c", j=PACK))
-        load_scale_rows(nc.sync, 0, w1_scales, range(2, 4))
+        load_scale_rows(nc.sync, 0, w1_scales, range(4))
         load_scale_rows(nc.sync, 4, w2_scales, range(2))
         nc.sync.dma_start(w1_raw[:], words_view(w1_words))
-        load_scale_rows(nc.sync, 4, w2_scales, range(2, 4))
         nc.sync.dma_start(w2_raw[:], words_view(w2_words))
+        load_scale_rows(nc.sync, 4, w2_scales, range(2, 4))
         load_scale_rows(nc.sync, 8, w5_scales, range(4))
         nc.sync.dma_start(w5_raw[:], words_view(w5_words))
 
@@ -186,6 +185,10 @@ def tile_picked_zshift_gelu_po_kernel(
 
         cast(nc.scalar.copy, w3_g, 0, w3_raw[:, :, 0:384])
         gather()
+        spare_bank = psum.tile([P, S], F32, name="spare_bank")
+        for t in range(PACK):
+            cols = slice(t * P, (t + 1) * P)
+            mm(spare_bank[:], xq_w[:, cols], xq_s[:, cols], xp_w[:], xp_s[:], True, True)
         cast(nc.vector.tensor_copy, w3_g, 96, w3_raw[:, :, 384:H])
         cast(nc.scalar.copy, w4_g, 0, w4_raw[:, :, 0:128])
         cast(nc.vector.tensor_copy, w4_g, 32, w4_raw[:, :, 128:H])

@@ -17,8 +17,11 @@ ALU = mybir.AluOpType
 
 P = 128
 PACK = 4
-HALF = 256
 CHUNK = 128
+CHUNKS = S // CHUNK
+W3_SCALAR = 336
+W4_SCALAR = 352
+WARM_PASSES = 3
 
 
 def tile_picked_zshift_gelu_po_kernel(
@@ -36,10 +39,10 @@ def tile_picked_zshift_gelu_po_kernel(
         def words_view(dram):
             return dram[0].rearrange("p n t -> p (n t)").bitcast(I32)
 
-        def load_scale_rows(queue, first, dram, quadrants):
+        def load_scale_rows(queue, plane, first, dram, quadrants):
             rows = dram[0].bitcast(I32)
             for q in quadrants:
-                queue.dma_start(ws_raw[32 * q + first : 32 * q + first + 4, :].bitcast(I32), rows[4 * q : 4 * q + 4, :])
+                queue.dma_start(plane[32 * q + first : 32 * q + first + 4, :].bitcast(I32), rows[4 * q : 4 * q + 4, :])
 
         offs_sb = sb.tile([P, S // 16], U16, name="offs_sb")
         prev_sb = sb.tile([P, S // 16], U16, name="prev_sb")
@@ -51,38 +54,39 @@ def tile_picked_zshift_gelu_po_kernel(
         w5_raw = tile("w5_raw", [P, N], I32)
         w3_raw = tile("w3_raw", [P, PACK, H], F32)
         w4_raw = tile("w4_raw", [P, PACK, H], F32)
-
         warm = tile("warm", [P, 2], F32)
-        nc.vector.memset(xs[:].bitcast(I32), 0)
+
+        def load_x_scales(queue, q):
+            rows = x_scales[0].bitcast(I32)[4 * q : 4 * q + 4, :]
+            queue.dma_start(xs[32 * q : 32 * q + 32, :].bitcast(I32), rows.partition_broadcast(8))
+
         nc.vector.memset(ws_raw[:].bitcast(I32), 0)
         nc.vector.memset(warm[:, 0:1], 0.0)
-        nc.scalar.activation(warm[:, 1:2], warm[:, 0:1], ACT.Gelu_apprx_tanh)
-        nc.sync.dma_start(xw[:], words_view(x_words))
         nc.sync.dma_start(offs_sb[:], offs)
-        nc.sync.dma_start(prev_sb[:], prev)
-        x_rows = x_scales[0].bitcast(I32)
         for q in range(4):
-            nc.sync.dma_start(xs[32 * q : 32 * q + 4, :].bitcast(I32), x_rows[4 * q : 4 * q + 4, :])
+            load_x_scales(nc.scalar if q < 2 else nc.sync, q)
+        nc.scalar.dma_start(xw[:], words_view(x_words))
+        nc.sync.dma_start(prev_sb[:], prev)
         nc.sync.dma_start(w3_raw[:], w3.rearrange("(p j) c -> p j c", j=PACK))
+        nc.scalar.activation(warm[:, 1:2], warm[:, 0:1], ACT.Gelu_apprx_tanh)
+        load_scale_rows(nc.gpsimd, ws_raw, 8, w5_scales, range(2))
+        load_scale_rows(nc.scalar, ws_raw, 0, w1_scales, range(4))
+        load_scale_rows(nc.sync, ws_raw, 4, w2_scales, range(2))
         nc.sync.dma_start(w4_raw[:], w4.rearrange("(p j) c -> p j c", j=PACK))
-        load_scale_rows(nc.sync, 0, w1_scales, range(4))
-        load_scale_rows(nc.sync, 4, w2_scales, range(2))
+        load_scale_rows(nc.sync, ws_raw, 4, w2_scales, range(2, 4))
+        load_scale_rows(nc.sync, ws_raw, 8, w5_scales, range(2, 4))
         nc.sync.dma_start(w1_raw[:], words_view(w1_words))
         nc.sync.dma_start(w2_raw[:], words_view(w2_words))
-        load_scale_rows(nc.sync, 4, w2_scales, range(2, 4))
-        load_scale_rows(nc.sync, 8, w5_scales, range(4))
         nc.sync.dma_start(w5_raw[:], words_view(w5_words))
 
         xq_w = tile("xq_w", [P, S], I32)
         xp_w = tile("xp_w", [P, S], I32)
         xq_s = tile("xq_s", [P, S], U8)
         xp_s = tile("xp_s", [P, S], U8)
-
-        def gather():
-            nc.vector.tensor_copy(xq_w[:].bitcast(U32), xw[:].bitcast(U32).indirect(offs_sb[:]))
-            nc.vector.tensor_copy(xp_w[:].bitcast(U32), xw[:].bitcast(U32).indirect(prev_sb[:]))
-            nc.vector.tensor_copy(xq_s[:], xs[:].indirect(offs_sb[:]))
-            nc.vector.tensor_copy(xp_s[:], xs[:].indirect(prev_sb[:]))
+        nc.vector.tensor_copy(xq_s[:], xs[:].indirect(offs_sb[:]))
+        nc.vector.tensor_copy(xp_s[:], xs[:].indirect(prev_sb[:]))
+        nc.vector.tensor_copy(xq_w[:].bitcast(U32), xw[:].bitcast(U32).indirect(offs_sb[:]))
+        nc.vector.tensor_copy(xp_w[:].bitcast(U32), xw[:].bitcast(U32).indirect(prev_sb[:]))
 
         def deal_words(name, raw, tag=None):
             dealt = tile(name, [P, N], I32, tag)
@@ -100,133 +104,129 @@ def tile_picked_zshift_gelu_po_kernel(
             )
             return dealt
 
-        def cast(copy, grouped, m0, raw):
-            ms = raw.shape[2] // PACK
+        def cast(copy, grouped, raw, c0, c1):
             copy(
-                grouped[:, :, m0 : m0 + ms, :].rearrange("p t m j -> p m t j"),
-                raw.rearrange("p j (m t) -> p m t j", t=PACK),
+                grouped[:, :, c0 // PACK : c1 // PACK, :].rearrange("p t m j -> p m t j"),
+                raw[:, :, c0:c1].rearrange("p j (m t) -> p m t j", t=PACK),
             )
 
-        def quantize(name, grouped, width, tags=(None, None)):
-            codes = tile(name + "_w", [P, width], I32, tags[0])
-            plane = tile(name + "_s", [P, width], U8, tags[1])
-            nc.vector.quantize_mx(out=codes[:].bitcast(FP8X4), scales=plane[:], in_=grouped)
+        def quantize(name, grouped, codes_tag=None, plane_tag=None):
+            codes = tile(name + "_w", [P, H], I32, codes_tag)
+            plane = tile(name + "_s", [P, H], U8, plane_tag)
+            nc.vector.quantize_mx(out=codes[:].bitcast(FP8X4), scales=plane[:], in_=grouped[:].rearrange("p t m j -> p (t m j)"))
             return codes, plane
 
         def mm(out, lw, ls, rw, rs, start, stop):
             nc.tensor.matmul_mx(out=out, lhsT=lw.bitcast(FP8X4), lhsT_scale=ls, rhs=rw.bitcast(FP8X4), rhs_scale=rs, start=start, stop=stop)
 
+        def tokens(c):
+            return slice(c * CHUNK, (c + 1) * CHUNK)
+
+        def passes(bank, words, plane, x_w, x_s, c, opens, closes):
+            for t in range(PACK):
+                cols = slice(t * P, (t + 1) * P)
+                mm(bank[:, t, :], words[:, cols], plane[:, cols], x_w[:, tokens(c)], x_s[:, tokens(c)],
+                   opens and t == 0, closes and t == PACK - 1)
+
         w3_g = tile("w3_g", [P, PACK, P, PACK], BF16)
         w4_g = tile("w4_g", [P, PACK, P, PACK], BF16)
-        gate = []
-
-        banks = [psum.tile([P, PACK, CHUNK], F32, name=f"bank{b}") for b in range(6)]
-        hy_bank = banks[0:4]
-        gate_bank = banks[2:6]
-
-        def gate_products(u):
-            tok = slice(u * HALF, (u + 1) * HALF)
-            gate.append(tile(f"gate{u}", [P, PACK, HALF], F32))
-            for pair in range(2):
-                bank = gate_bank[2 * u + pair][:].rearrange("p (e a) n -> p e (a n)", e=2)
-                for e in range(2):
-                    cols = slice((2 * pair + e) * P, (2 * pair + e + 1) * P)
-                    mm(bank[:, e, :], w1d[:, cols], ws[:, cols], xq_w[:, tok], xq_s[:, tok], True, False)
-                    mm(bank[:, e, :], w2d[:, cols], ws[4:, cols], xp_w[:, tok], xp_s[:, tok], False, True)
-                nc.scalar.activation(gate[u][:, 2 * pair : 2 * pair + 2, :], bank, ACT.Tanh, scale=0.5)
-
-        def gate_affine(u):
-            nc.vector.tensor_scalar(gate[u][:], gate[u][:], 0.5, 0.5, ALU.mult, ALU.add)
+        hy_bank = [psum.tile([P, PACK, CHUNK], F32, name=f"hy_bank{c}") for c in range(CHUNKS)]
+        gate_bank = [psum.tile([P, PACK, CHUNK], F32, name=f"gate_bank{c}") for c in range(CHUNKS - 1)]
+        gate_bank.append(gate_bank[1])
+        gate = [tile(f"gate{c}", [P, PACK, CHUNK], F32) for c in range(CHUNKS)]
+        h_g = [tile(f"h_g{c}", [P, CHUNK, PACK], BF16) for c in range(CHUNKS)]
+        h_w = tile("h_w", [P, S], I32)
+        h_s = tile("h_s", [P, S], U8)
 
         def hidden(c):
-            tok = slice(c * CHUNK, (c + 1) * CHUNK)
-            bank = hy_bank[c]
-            for t in range(PACK):
-                cols = slice(t * P, (t + 1) * P)
-                mm(bank[:, t, :], w3q[0][:, cols], w3q[1][:, cols], xq_w[:, tok], xq_s[:, tok], True, False)
-                mm(bank[:, t, :], w4q[0][:, cols], w4q[1][:, cols], xp_w[:, tok], xp_s[:, tok], False, True)
-            h_g = tile(f"h_g{c}", [P, CHUNK, PACK], BF16)
-            nc.scalar.activation(h_g[:], bank[:].rearrange("p t n -> p n t"), ACT.Gelu_apprx_tanh)
-            h_gs.append(h_g)
+            passes(hy_bank[c], w4q[0], w4q[1], xp_w, xp_s, c, False, True)
+            nc.scalar.activation(h_g[c][:], hy_bank[c][:].rearrange("p t n -> p n t"), ACT.Gelu_apprx_tanh)
 
         def hidden_codes(c):
-            tok = slice(c * CHUNK, (c + 1) * CHUNK)
-            nc.vector.quantize_mx(out=h_w[:, tok].bitcast(FP8X4), scales=h_s[:, tok], in_=h_gs[c][:].rearrange("p n t -> p (n t)"))
+            nc.vector.quantize_mx(out=h_w[:, tokens(c)].bitcast(FP8X4), scales=h_s[:, tokens(c)], in_=h_g[c][:].rearrange("p n t -> p (n t)"))
+
+        def gate_products(c):
+            passes(gate_bank[c], w1d, ws, xq_w, xq_s, c, True, False)
+            passes(gate_bank[c], w2d, ws[4:], xp_w, xp_s, c, False, True)
+            nc.scalar.activation(gate[c][:], gate_bank[c][:], ACT.Tanh, scale=0.5)
+
+        def halve(c):
+            flat = h_g[c][:].rearrange("p n t -> p (n t)")
+            nc.vector.tensor_scalar(flat, flat, 0.5, None, ALU.mult)
 
         def second(c):
-            tok = slice(c * CHUNK, (c + 1) * CHUNK)
-            bank = hy_bank[c]
-            for t in range(PACK):
-                cols = slice(t * P, (t + 1) * P)
-                mm(bank[:, t, :], w5d[:, cols], ws[8:, cols], h_w[:, tok], h_s[:, tok], True, True)
+            passes(hy_bank[c], w5d, ws[8:], h_w, h_s, c, True, True)
 
         out_rows = out_0.rearrange("(p t) n -> p t n", t=PACK)
         o_w = tile("o_w", [P, S], I32)
         o_s = tile("o_s", [P, S], U8)
-        pieces = [slice(0, 256), slice(256, 384), slice(384, 512)]
-        res = [tile(f"res{i}", [P, PACK, s.stop - s.start], F32) for i, s in enumerate(pieces)]
-        o_g = [tile(f"o_g{i}", [P, s.stop - s.start, PACK], BF16) for i, s in enumerate(pieces)]
+        res = [tile(f"res{c}", [P, PACK, CHUNK], F32) for c in range(CHUNKS)]
+        o_g = [tile(f"o_g{c}", [P, CHUNK, PACK], BF16) for c in range(CHUNKS)]
 
         def gated(c):
-            u, tok = c // 2, slice((c % 2) * CHUNK, (c % 2 + 1) * CHUNK)
-            dst = res[0][:, :, tok] if c < 2 else res[c - 1][:]
-            nc.vector.tensor_tensor(dst, hy_bank[c][:], gate[u][:, :, tok], ALU.mult)
+            nc.vector.scalar_tensor_tensor(res[c][:], gate[c][:], 1.0, hy_bank[c][:], ALU.add, ALU.mult)
+            nc.sync.dma_start(out_rows[:, :, tokens(c)], res[c][:])
 
-        def hand_out(i, copy):
-            nc.sync.dma_start(out_rows[:, :, pieces[i]], res[i][:])
-            copy(o_g[i][:], res[i][:].rearrange("p t n -> p n t"))
+        def round_out(c, copy):
+            copy(o_g[c][:].rearrange("p (a i) t -> p a t i", i=4), res[c][:].rearrange("p t (a i) -> p a t i", i=4))
 
-        def planes(i):
+        def planes(c):
             nc.vector.quantize_mx(
-                out=o_w[:, pieces[i]].bitcast(FP8X4),
-                scales=o_s[:, pieces[i]],
-                in_=o_g[i][:].rearrange("p n t -> p (n t)"),
+                out=o_w[:, tokens(c)].bitcast(FP8X4), scales=o_s[:, tokens(c)], in_=o_g[c][:].rearrange("p n t -> p (n t)")
             )
 
-        cast(nc.scalar.copy, w3_g, 0, w3_raw[:, :, 0:384])
-        gather()
         spare_bank = psum.tile([P, S], F32, name="spare_bank")
-        for t in range(PACK):
+        for t in range(WARM_PASSES):
             cols = slice(t * P, (t + 1) * P)
-            mm(spare_bank[:], xq_w[:, cols], xq_s[:, cols], xp_w[:], xp_s[:], True, True)
-        cast(nc.vector.tensor_copy, w3_g, 96, w3_raw[:, :, 384:H])
-        cast(nc.scalar.copy, w4_g, 0, w4_raw[:, :, 0:128])
-        cast(nc.vector.tensor_copy, w4_g, 32, w4_raw[:, :, 128:H])
-        w3q = quantize("w3q", w3_g[:].rearrange("p t m j -> p (t m j)"), H, ("w4_raw", None))
-        w4q = quantize("w4q", w4_g[:].rearrange("p t m j -> p (t m j)"), H)
-        h_gs = []
+            mm(spare_bank[:], xq_w[:, cols], xq_s[:, cols], xq_w[:], xq_s[:], True, True)
+        cast(nc.scalar.copy, w3_g, w3_raw, 0, W3_SCALAR)
+        cast(nc.vector.tensor_copy, w3_g, w3_raw, W3_SCALAR, H)
+        w3q = quantize("w3q", w3_g)
+        cast(nc.scalar.copy, w4_g, w4_raw, 0, W4_SCALAR)
+        cast(nc.vector.tensor_copy, w4_g, w4_raw, W4_SCALAR, H)
+        w1d = deal_words("w1d", w1_raw)
+        ws = deal_scales("ws", ws_raw)
+        w2d = deal_words("w2d", w2_raw)
+        w4q = quantize("w4q", w4_g, "w2_raw", "ws_raw")
+        w5d = deal_words("w5d", w5_raw)
+        for c in range(CHUNKS):
+            passes(hy_bank[c], w3q[0], w3q[1], xq_w, xq_s, c, True, False)
+        gate_products(0)
         hidden(0)
         hidden(1)
-        w1d = deal_words("w1d", w1_raw, "w4_g")
-        w2d = deal_words("w2d", w2_raw, "w1_raw")
-        ws = deal_scales("ws", ws_raw, "w2_raw")
-        w5d = deal_words("w5d", w5_raw, "ws_raw")
-        h_w = tile("h_w", [P, S], I32)
-        h_s = tile("h_s", [P, S], U8, "w5_raw")
+        halve(0)
+        hidden(2)
+        halve(1)
         hidden_codes(0)
+        second(0)
+        hidden(3)
+        halve(2)
         hidden_codes(1)
-        gate_products(0)
+        second(1)
         gate_products(1)
-        gate_affine(0)
-        gate_affine(1)
-        for c in range(2):
-            hidden(c + 2)
-            second(c)
-            hidden_codes(c + 2)
-        gated(0)
-        gated(1)
-        hand_out(0, nc.scalar.copy)
+        halve(3)
+        hidden_codes(2)
         second(2)
-        gated(2)
-        hand_out(1, nc.scalar.copy)
+        gated(0)
+        gate_products(2)
+        hidden_codes(3)
         second(3)
+        gate_products(3)
+        gated(1)
+        round_out(0, nc.scalar.copy)
+        gated(2)
+        round_out(1, nc.scalar.copy)
         gated(3)
+        round_out(2, nc.vector.tensor_copy)
         planes(0)
-        hand_out(2, nc.vector.tensor_copy)
-        planes(1)
+        round_out(3, nc.vector.tensor_copy)
         planes(2)
-        nc.scalar.dma_start(words_view(out_1), o_w[:])
+        planes(1)
+        head = (CHUNKS - 1) * CHUNK
+        nc.sync.dma_start(words_view(out_1)[:, 0:head], o_w[:, 0:head])
+        planes(3)
+        nc.sync.dma_start(words_view(out_1)[:, head:S], o_w[:, head:S])
         scale_rows = out_2[0].bitcast(I32)
         for q in range(4):
-            queue = nc.sync if q % 2 == 0 else nc.scalar
+            queue = nc.scalar if q % 2 == 0 else nc.sync
             queue.dma_start(scale_rows[4 * q : 4 * q + 4, :], o_s[32 * q : 32 * q + 4, :].bitcast(I32))

@@ -18,6 +18,7 @@ ALU = mybir.AluOpType
 P = 128
 PACK = 4
 CHUNK = 128
+HALF = 256
 CHUNKS = S // CHUNK
 W3_SCALAR = 336
 W4_SCALAR = 352
@@ -73,10 +74,10 @@ def tile_picked_zshift_gelu_po_kernel(
         load_scale_rows(nc.scalar, ws_raw, 0, w1_scales, range(4))
         load_scale_rows(nc.sync, ws_raw, 4, w2_scales, range(2))
         nc.sync.dma_start(w4_raw[:], w4.rearrange("(p j) c -> p j c", j=PACK))
-        load_scale_rows(nc.sync, ws_raw, 4, w2_scales, range(2, 4))
-        load_scale_rows(nc.sync, ws_raw, 8, w5_scales, range(2, 4))
         nc.sync.dma_start(w1_raw[:], words_view(w1_words))
         nc.sync.dma_start(w2_raw[:], words_view(w2_words))
+        load_scale_rows(nc.sync, ws_raw, 4, w2_scales, range(2, 4))
+        load_scale_rows(nc.sync, ws_raw, 8, w5_scales, range(2, 4))
         nc.sync.dma_start(w5_raw[:], words_view(w5_words))
 
         xq_w = tile("xq_w", [P, S], I32)
@@ -122,75 +123,89 @@ def tile_picked_zshift_gelu_po_kernel(
         def tokens(c):
             return slice(c * CHUNK, (c + 1) * CHUNK)
 
-        def passes(bank, words, plane, x_w, x_s, c, opens, closes):
-            for t in range(PACK):
-                cols = slice(t * P, (t + 1) * P)
-                mm(bank[:, t, :], words[:, cols], plane[:, cols], x_w[:, tokens(c)], x_s[:, tokens(c)],
-                   opens and t == 0, closes and t == PACK - 1)
+        def passes(outs, first, words, plane, x_w, x_s, tok, opens, closes):
+            for e, out in enumerate(outs):
+                cols = slice((first + e) * P, (first + e + 1) * P)
+                mm(out, words[:, cols], plane[:, cols], x_w[:, tok], x_s[:, tok], opens and e == 0, closes and e == len(outs) - 1)
+
+        def by_chunk(bank):
+            return [bank[:, t * CHUNK : (t + 1) * CHUNK] for t in range(PACK)]
+
+        def by_half(bank):
+            return [bank[:, e * HALF : (e + 1) * HALF] for e in range(2)]
+
+        def half_tokens(u):
+            return slice(u * HALF, (u + 1) * HALF)
 
         w3_g = tile("w3_g", [P, PACK, P, PACK], BF16)
         w4_g = tile("w4_g", [P, PACK, P, PACK], BF16)
-        hy_bank = [psum.tile([P, PACK, CHUNK], F32, name=f"hy_bank{c}") for c in range(CHUNKS)]
-        gate_bank = [psum.tile([P, PACK, CHUNK], F32, name=f"gate_bank{c}") for c in range(CHUNKS - 1)]
-        gate_bank.append(gate_bank[1])
-        gate = [tile(f"gate{c}", [P, PACK, CHUNK], F32) for c in range(CHUNKS)]
+        hy_bank = [psum.tile([P, S], F32, name=f"hy_bank{b}") for b in range(4)]
+        gate_bank = [psum.tile([P, S], F32, name=f"gate_bank{b}") for b in range(4)]
+        gate = [tile(f"gate{b}", [P, S], F32) for b in range(4)]
         h_g = [tile(f"h_g{c}", [P, CHUNK, PACK], BF16) for c in range(CHUNKS)]
         h_w = tile("h_w", [P, S], I32)
         h_s = tile("h_s", [P, S], U8)
 
         def hidden(c):
-            passes(hy_bank[c], w4q[0], w4q[1], xp_w, xp_s, c, False, True)
-            nc.scalar.activation(h_g[c][:], hy_bank[c][:].rearrange("p t n -> p n t"), ACT.Gelu_apprx_tanh)
-
-        def hidden_codes(c):
-            nc.vector.quantize_mx(out=h_w[:, tokens(c)].bitcast(FP8X4), scales=h_s[:, tokens(c)], in_=h_g[c][:].rearrange("p n t -> p (n t)"))
-
-        def gate_products(c):
-            passes(gate_bank[c], w1d, ws, xq_w, xq_s, c, True, False)
-            passes(gate_bank[c], w2d, ws[4:], xp_w, xp_s, c, False, True)
-            nc.scalar.activation(gate[c][:], gate_bank[c][:], ACT.Tanh, scale=0.5)
+            passes(by_chunk(hy_bank[c]), 0, w4q[0], w4q[1], xp_w, xp_s, tokens(c), False, True)
+            nc.scalar.activation(h_g[c][:], hy_bank[c][:].rearrange("p (t n) -> p n t", t=PACK), ACT.Gelu_apprx_tanh)
 
         def halve(c):
             flat = h_g[c][:].rearrange("p n t -> p (n t)")
             nc.vector.tensor_scalar(flat, flat, 0.5, None, ALU.mult)
 
-        def second(c):
-            passes(hy_bank[c], w5d, ws[8:], h_w, h_s, c, True, True)
+        def hidden_codes(c):
+            nc.vector.quantize_mx(out=h_w[:, tokens(c)].bitcast(FP8X4), scales=h_s[:, tokens(c)], in_=h_g[c][:].rearrange("p n t -> p (n t)"))
+
+        def gate_products(b):
+            u, pair = divmod(b, 2)
+            passes(by_half(gate_bank[b]), 2 * pair, w1d, ws, xq_w, xq_s, half_tokens(u), True, False)
+            passes(by_half(gate_bank[b]), 2 * pair, w2d, ws[4:], xp_w, xp_s, half_tokens(u), False, True)
+            nc.scalar.activation(gate[b][:], gate_bank[b][:], ACT.Tanh, scale=0.5)
+
+        def second(b):
+            u, pair = divmod(b, 2)
+            passes(by_half(hy_bank[b]), 2 * pair, w5d, ws[8:], h_w, h_s, half_tokens(u), True, True)
 
         out_rows = out_0.rearrange("(p t) n -> p t n", t=PACK)
         o_w = tile("o_w", [P, S], I32)
-        o_s = tile("o_s", [P, S], U8)
-        res = [tile(f"res{c}", [P, PACK, CHUNK], F32) for c in range(CHUNKS)]
-        o_g = [tile(f"o_g{c}", [P, CHUNK, PACK], BF16) for c in range(CHUNKS)]
+        res = [tile(f"res{u}", [P, PACK, HALF], F32) for u in range(2)]
+        o_g = tile("o_g", [P, S, PACK], BF16)
 
-        def gated(c):
-            nc.vector.scalar_tensor_tensor(res[c][:], gate[c][:], 1.0, hy_bank[c][:], ALU.add, ALU.mult)
-            nc.sync.dma_start(out_rows[:, :, tokens(c)], res[c][:])
+        def gated(b):
+            u, pair = divmod(b, 2)
+            piece = res[u][:, 2 * pair : 2 * pair + 2, :]
+            nc.vector.scalar_tensor_tensor(piece.rearrange("p t n -> p (t n)"), gate[b][:], 1.0, hy_bank[b][:], ALU.add, ALU.mult)
+            nc.sync.dma_start(out_rows[:, 2 * pair : 2 * pair + 2, half_tokens(u)], piece)
 
         def round_out(c, copy):
-            copy(o_g[c][:].rearrange("p (a i) t -> p a t i", i=4), res[c][:].rearrange("p t (a i) -> p a t i", i=4))
-
-        def planes(c):
-            nc.vector.quantize_mx(
-                out=o_w[:, tokens(c)].bitcast(FP8X4), scales=o_s[:, tokens(c)], in_=o_g[c][:].rearrange("p n t -> p (n t)")
+            u, part = divmod(c, 2)
+            copy(
+                o_g[:, tokens(c), :].rearrange("p (a i) t -> p a t i", i=4),
+                res[u][:, :, tokens(part)].rearrange("p t (a i) -> p a t i", i=4),
             )
 
-        spare_bank = psum.tile([P, S], F32, name="spare_bank")
+        def planes(u):
+            tok = half_tokens(u)
+            nc.vector.quantize_mx(
+                out=o_w[:, tok].bitcast(FP8X4), scales=o_s[:, tok], in_=o_g[:, tok, :].rearrange("p n t -> p (n t)")
+            )
+
         for t in range(WARM_PASSES):
             cols = slice(t * P, (t + 1) * P)
-            mm(spare_bank[:], xq_w[:, cols], xq_s[:, cols], xq_w[:], xq_s[:], True, True)
+            mm(gate_bank[3][:], xq_w[:, cols], xq_s[:, cols], xq_w[:], xq_s[:], True, True)
         cast(nc.scalar.copy, w3_g, w3_raw, 0, W3_SCALAR)
         cast(nc.vector.tensor_copy, w3_g, w3_raw, W3_SCALAR, H)
         w3q = quantize("w3q", w3_g)
         cast(nc.scalar.copy, w4_g, w4_raw, 0, W4_SCALAR)
         cast(nc.vector.tensor_copy, w4_g, w4_raw, W4_SCALAR, H)
         w1d = deal_words("w1d", w1_raw)
-        ws = deal_scales("ws", ws_raw)
         w2d = deal_words("w2d", w2_raw)
+        ws = deal_scales("ws", ws_raw)
         w4q = quantize("w4q", w4_g, "w2_raw", "ws_raw")
         w5d = deal_words("w5d", w5_raw)
         for c in range(CHUNKS):
-            passes(hy_bank[c], w3q[0], w3q[1], xq_w, xq_s, c, True, False)
+            passes(by_chunk(hy_bank[c]), 0, w3q[0], w3q[1], xq_w, xq_s, tokens(c), True, False)
         gate_products(0)
         hidden(0)
         hidden(1)
@@ -198,34 +213,30 @@ def tile_picked_zshift_gelu_po_kernel(
         hidden(2)
         halve(1)
         hidden_codes(0)
-        second(0)
         hidden(3)
-        halve(2)
         hidden_codes(1)
+        second(0)
         second(1)
+        halve(2)
         gate_products(1)
+        gate_products(2)
         halve(3)
         hidden_codes(2)
-        second(2)
-        gated(0)
-        gate_products(2)
         hidden_codes(3)
-        second(3)
         gate_products(3)
-        gated(1)
+        second(2)
+        second(3)
+        for b in range(4):
+            gated(b)
         round_out(0, nc.scalar.copy)
-        gated(2)
         round_out(1, nc.scalar.copy)
-        gated(3)
+        o_s = tile("o_s", [P, S], U8, "gate3")
         round_out(2, nc.vector.tensor_copy)
+        round_out(3, nc.scalar.copy)
         planes(0)
-        round_out(3, nc.vector.tensor_copy)
-        planes(2)
+        nc.sync.dma_start(words_view(out_1)[:, 0:HALF], o_w[:, 0:HALF])
         planes(1)
-        head = (CHUNKS - 1) * CHUNK
-        nc.sync.dma_start(words_view(out_1)[:, 0:head], o_w[:, 0:head])
-        planes(3)
-        nc.sync.dma_start(words_view(out_1)[:, head:S], o_w[:, head:S])
+        nc.scalar.dma_start(words_view(out_1)[:, HALF:S], o_w[:, HALF:S])
         scale_rows = out_2[0].bitcast(I32)
         for q in range(4):
             queue = nc.scalar if q % 2 == 0 else nc.sync

@@ -21,8 +21,9 @@ CHUNK = 128
 HALF = 256
 CHUNKS = S // CHUNK
 W3_SCALAR = 336
-W4_SCALAR = 352
-WARM_PASSES = 3
+W4_SCALAR = 224
+WARM_EARLY = 2
+WARM_LATE = 3
 
 
 def tile_picked_zshift_gelu_po_kernel(
@@ -142,20 +143,20 @@ def tile_picked_zshift_gelu_po_kernel(
         hy_bank = [psum.tile([P, S], F32, name=f"hy_bank{b}") for b in range(4)]
         gate_bank = [psum.tile([P, S], F32, name=f"gate_bank{b}") for b in range(4)]
         gate = [tile(f"gate{b}", [P, S], F32) for b in range(4)]
-        h_g = [tile(f"h_g{c}", [P, CHUNK, PACK], BF16) for c in range(CHUNKS)]
+        h_g = {}
         h_w = tile("h_w", [P, S], I32)
         h_s = tile("h_s", [P, S], U8)
 
         def hidden(c):
             passes(by_chunk(hy_bank[c]), 0, w4q[0], w4q[1], xp_w, xp_s, tokens(c), False, True)
+            h_g[c] = tile(f"h_g{c}", [P, CHUNK, PACK], BF16, f"h_g{c % (CHUNKS - 1)}")
             nc.scalar.activation(h_g[c][:], hy_bank[c][:].rearrange("p (t n) -> p n t", t=PACK), ACT.Gelu_apprx_tanh)
 
         def halve(c):
-            flat = h_g[c][:].rearrange("p n t -> p (n t)")
-            nc.vector.tensor_scalar(flat, flat, 0.5, None, ALU.mult)
+            nc.vector.tensor_scalar(h_half[:, tokens(c), :], h_g[c][:], 0.5, None, ALU.mult)
 
         def hidden_codes(c):
-            nc.vector.quantize_mx(out=h_w[:, tokens(c)].bitcast(FP8X4), scales=h_s[:, tokens(c)], in_=h_g[c][:].rearrange("p n t -> p (n t)"))
+            nc.vector.quantize_mx(out=h_w[:, tokens(c)].bitcast(FP8X4), scales=h_s[:, tokens(c)], in_=h_half[:, tokens(c), :].rearrange("p n t -> p (n t)"))
 
         def gate_products(b):
             u, pair = divmod(b, 2)
@@ -170,7 +171,6 @@ def tile_picked_zshift_gelu_po_kernel(
         out_rows = out_0.rearrange("(p t) n -> p t n", t=PACK)
         o_w = tile("o_w", [P, S], I32)
         res = [tile(f"res{u}", [P, PACK, HALF], F32) for u in range(2)]
-        o_g = tile("o_g", [P, S, PACK], BF16)
 
         def gated(b):
             u, pair = divmod(b, 2)
@@ -191,43 +191,42 @@ def tile_picked_zshift_gelu_po_kernel(
                 out=o_w[:, tok].bitcast(FP8X4), scales=o_s[:, tok], in_=o_g[:, tok, :].rearrange("p n t -> p (n t)")
             )
 
-        for t in range(WARM_PASSES):
-            cols = slice(t * P, (t + 1) * P)
-            mm(gate_bank[3][:], xq_w[:, cols], xq_s[:, cols], xq_w[:], xq_s[:], True, True)
+        for moving_w, moving_s, count in ((xq_w, xq_s, WARM_EARLY), (xp_w, xp_s, WARM_LATE)):
+            for t in range(count):
+                cols = slice(t * P, (t + 1) * P)
+                mm(gate_bank[3][:], xq_w[:, cols], xq_s[:, cols], moving_w[:], moving_s[:], True, True)
         cast(nc.scalar.copy, w3_g, w3_raw, 0, W3_SCALAR)
         cast(nc.vector.tensor_copy, w3_g, w3_raw, W3_SCALAR, H)
         w3q = quantize("w3q", w3_g)
         cast(nc.scalar.copy, w4_g, w4_raw, 0, W4_SCALAR)
         cast(nc.vector.tensor_copy, w4_g, w4_raw, W4_SCALAR, H)
-        w1d = deal_words("w1d", w1_raw)
+        w4q = quantize("w4q", w4_g)
+        w1d = deal_words("w1d", w1_raw, "w4_g")
         w2d = deal_words("w2d", w2_raw)
         ws = deal_scales("ws", ws_raw)
-        w4q = quantize("w4q", w4_g, "w2_raw", "ws_raw")
         w5d = deal_words("w5d", w5_raw)
+        h_half = tile("h_half", [P, S, PACK], BF16, "ws_raw")
         for c in range(CHUNKS):
             passes(by_chunk(hy_bank[c]), 0, w3q[0], w3q[1], xq_w, xq_s, tokens(c), True, False)
+        for c in range(CHUNKS - 1):
+            hidden(c)
         gate_products(0)
-        hidden(0)
-        hidden(1)
-        halve(0)
-        hidden(2)
-        halve(1)
-        hidden_codes(0)
-        hidden(3)
-        hidden_codes(1)
+        for c in range(CHUNKS - 1):
+            halve(c)
+            hidden_codes(c)
+        hidden(CHUNKS - 1)
+        halve(CHUNKS - 1)
+        hidden_codes(CHUNKS - 1)
         second(0)
-        second(1)
-        halve(2)
         gate_products(1)
+        second(1)
         gate_products(2)
-        halve(3)
-        hidden_codes(2)
-        hidden_codes(3)
         gate_products(3)
         second(2)
         second(3)
         for b in range(4):
             gated(b)
+        o_g = tile("o_g", [P, S, PACK], BF16, "w2d")
         round_out(0, nc.scalar.copy)
         round_out(1, nc.scalar.copy)
         o_s = tile("o_s", [P, S], U8, "gate3")

@@ -20,10 +20,9 @@ PACK = 4
 CHUNK = 128
 HALF = 256
 CHUNKS = S // CHUNK
-W3_SCALAR = 336
-W4_SCALAR = 224
-WARM_EARLY = 2
-WARM_LATE = 3
+W4_SCALAR = 320
+WARM_EARLY = 3
+WARM_LATE = 2
 
 
 def tile_picked_zshift_gelu_po_kernel(
@@ -41,44 +40,44 @@ def tile_picked_zshift_gelu_po_kernel(
         def words_view(dram):
             return dram[0].rearrange("p n t -> p (n t)").bitcast(I32)
 
-        def load_scale_rows(queue, plane, first, dram, quadrants):
-            rows = dram[0].bitcast(I32)
-            for q in quadrants:
-                queue.dma_start(plane[32 * q + first : 32 * q + first + 4, :].bitcast(I32), rows[4 * q : 4 * q + 4, :])
-
         offs_sb = sb.tile([P, S // 16], U16, name="offs_sb")
         prev_sb = sb.tile([P, S // 16], U16, name="prev_sb")
         xw = tile("xw", [P, T], I32)
         xs = tile("xs", [P, T], U8)
+        ws_stage = tile("ws_stage", [P, N], U8)
         ws_raw = tile("ws_raw", [P, N], U8)
         w1_raw = tile("w1_raw", [P, N], I32)
         w2_raw = tile("w2_raw", [P, N], I32)
         w5_raw = tile("w5_raw", [P, N], I32)
-        w3_raw = tile("w3_raw", [P, PACK, H], F32)
-        w4_raw = tile("w4_raw", [P, PACK, H], F32)
+        w3_raw = [tile(f"w3_raw{u}", [P, PACK, HALF], F32) for u in range(2)]
+        w4_raw = [tile(f"w4_raw{u}", [P, PACK, HALF], F32) for u in range(2)]
         warm = tile("warm", [P, 2], F32)
 
         def load_x_scales(queue, q):
             rows = x_scales[0].bitcast(I32)[4 * q : 4 * q + 4, :]
             queue.dma_start(xs[32 * q : 32 * q + 32, :].bitcast(I32), rows.partition_broadcast(8))
 
-        nc.vector.memset(ws_raw[:].bitcast(I32), 0)
+        def load_half(raw, dram, u):
+            nc.sync.dma_start(raw[u][:], dram.rearrange("(p j) c -> p j c", j=PACK)[:, :, u * HALF : (u + 1) * HALF])
+
         nc.vector.memset(warm[:, 0:1], 0.0)
+        nc.vector.memset(ws_stage[:].bitcast(I32), 0)
         nc.sync.dma_start(offs_sb[:], offs)
         for q in range(4):
             load_x_scales(nc.scalar if q < 2 else nc.sync, q)
-        nc.scalar.dma_start(xw[:], words_view(x_words))
+        nc.sync.dma_start(xw[:], words_view(x_words))
         nc.sync.dma_start(prev_sb[:], prev)
-        nc.sync.dma_start(w3_raw[:], w3.rearrange("(p j) c -> p j c", j=PACK))
         nc.scalar.activation(warm[:, 1:2], warm[:, 0:1], ACT.Gelu_apprx_tanh)
-        load_scale_rows(nc.gpsimd, ws_raw, 8, w5_scales, range(2))
-        load_scale_rows(nc.scalar, ws_raw, 0, w1_scales, range(4))
-        load_scale_rows(nc.sync, ws_raw, 4, w2_scales, range(2))
-        nc.sync.dma_start(w4_raw[:], w4.rearrange("(p j) c -> p j c", j=PACK))
+        load_half(w3_raw, w3, 0)
+        for w, dram in enumerate((w1_scales, w2_scales, w5_scales)):
+            nc.sync.dma_start(ws_stage[16 * w : 16 * w + 16, :].bitcast(I32), dram[0].bitcast(I32).rearrange("(q r) c -> r q c", r=4))
+        load_half(w3_raw, w3, 1)
+        for u in range(2):
+            load_half(w4_raw, w4, u)
         nc.sync.dma_start(w1_raw[:], words_view(w1_words))
         nc.sync.dma_start(w2_raw[:], words_view(w2_words))
-        load_scale_rows(nc.sync, ws_raw, 4, w2_scales, range(2, 4))
-        load_scale_rows(nc.sync, ws_raw, 8, w5_scales, range(2, 4))
+        for q in range(4):
+            nc.sync.dma_start(ws_raw[32 * q : 32 * q + 32, :].bitcast(I32), ws_stage[q:P:4, :].bitcast(I32))
         nc.sync.dma_start(w5_raw[:], words_view(w5_words))
 
         xq_w = tile("xq_w", [P, S], I32)
@@ -86,8 +85,8 @@ def tile_picked_zshift_gelu_po_kernel(
         xq_s = tile("xq_s", [P, S], U8)
         xp_s = tile("xp_s", [P, S], U8)
         nc.vector.tensor_copy(xq_s[:], xs[:].indirect(offs_sb[:]))
-        nc.vector.tensor_copy(xp_s[:], xs[:].indirect(prev_sb[:]))
         nc.vector.tensor_copy(xq_w[:].bitcast(U32), xw[:].bitcast(U32).indirect(offs_sb[:]))
+        nc.vector.tensor_copy(xp_s[:], xs[:].indirect(prev_sb[:]))
         nc.vector.tensor_copy(xp_w[:].bitcast(U32), xw[:].bitcast(U32).indirect(prev_sb[:]))
 
         def deal_words(name, raw, tag=None):
@@ -109,7 +108,7 @@ def tile_picked_zshift_gelu_po_kernel(
         def cast(copy, grouped, raw, c0, c1):
             copy(
                 grouped[:, :, c0 // PACK : c1 // PACK, :].rearrange("p t m j -> p m t j"),
-                raw[:, :, c0:c1].rearrange("p j (m t) -> p m t j", t=PACK),
+                raw[c0 // HALF][:, :, c0 % HALF : c0 % HALF + c1 - c0].rearrange("p j (m t) -> p m t j", t=PACK),
             )
 
         def quantize(name, grouped, codes_tag=None, plane_tag=None):
@@ -195,13 +194,14 @@ def tile_picked_zshift_gelu_po_kernel(
             for t in range(count):
                 cols = slice(t * P, (t + 1) * P)
                 mm(gate_bank[3][:], xq_w[:, cols], xq_s[:, cols], moving_w[:], moving_s[:], True, True)
-        cast(nc.scalar.copy, w3_g, w3_raw, 0, W3_SCALAR)
-        cast(nc.vector.tensor_copy, w3_g, w3_raw, W3_SCALAR, H)
+        cast(nc.scalar.copy, w3_g, w3_raw, 0, HALF)
+        cast(nc.scalar.copy, w3_g, w3_raw, HALF, H)
         w3q = quantize("w3q", w3_g)
-        cast(nc.scalar.copy, w4_g, w4_raw, 0, W4_SCALAR)
+        cast(nc.scalar.copy, w4_g, w4_raw, 0, HALF)
+        cast(nc.scalar.copy, w4_g, w4_raw, HALF, W4_SCALAR)
         cast(nc.vector.tensor_copy, w4_g, w4_raw, W4_SCALAR, H)
         w4q = quantize("w4q", w4_g)
-        w1d = deal_words("w1d", w1_raw, "w4_g")
+        w1d = deal_words("w1d", w1_raw, "w4_raw1")
         w2d = deal_words("w2d", w2_raw)
         ws = deal_scales("ws", ws_raw)
         w5d = deal_words("w5d", w5_raw)

@@ -107,8 +107,8 @@ def tile_picked_zshift_gelu_po_kernel(
 
         def cast(copy, grouped, raw, c0, c1):
             copy(
-                grouped[:, :, c0 // PACK : c1 // PACK, :].rearrange("p t m j -> p m t j"),
-                raw[c0 // HALF][:, :, c0 % HALF : c0 % HALF + c1 - c0].rearrange("p j (m t) -> p m t j", t=PACK),
+                grouped[:, :, c0 // PACK : c1 // PACK, :].rearrange("p t m j -> p m j t"),
+                raw[c0 // HALF][:, :, c0 % HALF : c0 % HALF + c1 - c0].rearrange("p j (m t) -> p m j t", t=PACK),
             )
 
         def quantize(name, grouped, codes_tag=None, plane_tag=None):

@@ -20,9 +20,9 @@ PACK = 4
 CHUNK = 128
 HALF = 256
 CHUNKS = S // CHUNK
-W4_SCALAR = 320
-WARM_EARLY = 3
-WARM_LATE = 2
+ROUND_VECTOR = 160
+LAST_SCALAR = 40
+WARM = 4
 
 
 def tile_picked_zshift_gelu_po_kernel(
@@ -105,17 +105,16 @@ def tile_picked_zshift_gelu_po_kernel(
             )
             return dealt
 
-        def cast(copy, grouped, raw, c0, c1):
+        def cast(copy, grouped, raw, u, t0, m0=0, m1=HALF // PACK):
+            first = u * HALF // PACK
             copy(
-                grouped[:, :, c0 // PACK : c1 // PACK, :].rearrange("p t m j -> p m j t"),
-                raw[c0 // HALF][:, :, c0 % HALF : c0 % HALF + c1 - c0].rearrange("p j (m t) -> p m j t", t=PACK),
+                grouped[:, :, first + m0 : first + m1, :].rearrange("p t m j -> p m j t"),
+                raw[u][:].rearrange("p j (m t) -> p m j t", t=PACK)[:, m0:m1, :, t0 : t0 + grouped.shape[1]],
             )
 
-        def quantize(name, grouped, codes_tag=None, plane_tag=None):
-            codes = tile(name + "_w", [P, H], I32, codes_tag)
-            plane = tile(name + "_s", [P, H], U8, plane_tag)
-            nc.vector.quantize_mx(out=codes[:].bitcast(FP8X4), scales=plane[:], in_=grouped[:].rearrange("p t m j -> p (t m j)"))
-            return codes, plane
+        def quantize(codes, plane, grouped, t0):
+            cols = slice(t0 * P, (t0 + grouped.shape[1]) * P)
+            nc.vector.quantize_mx(out=codes[:, cols].bitcast(FP8X4), scales=plane[:, cols], in_=grouped.rearrange("p t m j -> p (t m j)"))
 
         def mm(out, lw, ls, rw, rs, start, stop):
             nc.tensor.matmul_mx(out=out, lhsT=lw.bitcast(FP8X4), lhsT_scale=ls, rhs=rw.bitcast(FP8X4), rhs_scale=rs, start=start, stop=stop)
@@ -138,27 +137,31 @@ def tile_picked_zshift_gelu_po_kernel(
             return slice(u * HALF, (u + 1) * HALF)
 
         w3_g = tile("w3_g", [P, PACK, P, PACK], BF16)
-        w4_g = tile("w4_g", [P, PACK, P, PACK], BF16)
+        w4_g = [tile(f"w4_g{pair}", [P, 2, P, PACK], BF16) for pair in range(2)]
         hy_bank = [psum.tile([P, S], F32, name=f"hy_bank{b}") for b in range(4)]
-        gate_bank = [psum.tile([P, S], F32, name=f"gate_bank{b}") for b in range(4)]
+        warm_bank = psum.tile([P, S], F32, name="warm_bank")
+        gate_bank = {}
         gate = [tile(f"gate{b}", [P, S], F32) for b in range(4)]
         h_g = {}
+        h_half = {}
         h_w = tile("h_w", [P, S], I32)
         h_s = tile("h_s", [P, S], U8)
 
         def hidden(c):
             passes(by_chunk(hy_bank[c]), 0, w4q[0], w4q[1], xp_w, xp_s, tokens(c), False, True)
-            h_g[c] = tile(f"h_g{c}", [P, CHUNK, PACK], BF16, f"h_g{c % (CHUNKS - 1)}")
+            h_g[c] = tile(f"h_g{c}", [P, CHUNK, PACK], BF16, f"h_g{c}")
             nc.scalar.activation(h_g[c][:], hy_bank[c][:].rearrange("p (t n) -> p n t", t=PACK), ACT.Gelu_apprx_tanh)
 
         def halve(c):
-            nc.vector.tensor_scalar(h_half[:, tokens(c), :], h_g[c][:], 0.5, None, ALU.mult)
+            h_half[c] = tile(f"h_half{c}", [P, CHUNK, PACK], BF16, ("ws_raw", "w5_raw")[c % 2])
+            nc.vector.tensor_scalar(h_half[c][:], h_g[c][:], 0.5, None, ALU.mult)
 
         def hidden_codes(c):
-            nc.vector.quantize_mx(out=h_w[:, tokens(c)].bitcast(FP8X4), scales=h_s[:, tokens(c)], in_=h_half[:, tokens(c), :].rearrange("p n t -> p (n t)"))
+            nc.vector.quantize_mx(out=h_w[:, tokens(c)].bitcast(FP8X4), scales=h_s[:, tokens(c)], in_=h_half[c][:].rearrange("p n t -> p (n t)"))
 
         def gate_products(b):
             u, pair = divmod(b, 2)
+            gate_bank[b] = psum.tile([P, S], F32, name=f"gate_bank{b}", tag=f"gate_bank{b % 3}")
             passes(by_half(gate_bank[b]), 2 * pair, w1d, ws, xq_w, xq_s, half_tokens(u), True, False)
             passes(by_half(gate_bank[b]), 2 * pair, w2d, ws[4:], xp_w, xp_s, half_tokens(u), False, True)
             nc.scalar.activation(gate[b][:], gate_bank[b][:], ACT.Tanh, scale=0.5)
@@ -177,11 +180,10 @@ def tile_picked_zshift_gelu_po_kernel(
             nc.vector.scalar_tensor_tensor(piece.rearrange("p t n -> p (t n)"), gate[b][:], 1.0, hy_bank[b][:], ALU.add, ALU.mult)
             nc.sync.dma_start(out_rows[:, 2 * pair : 2 * pair + 2, half_tokens(u)], piece)
 
-        def round_out(c, copy):
-            u, part = divmod(c, 2)
+        def round_out(copy, u, n0, n1):
             copy(
-                o_g[:, tokens(c), :].rearrange("p (a i) t -> p a t i", i=4),
-                res[u][:, :, tokens(part)].rearrange("p t (a i) -> p a t i", i=4),
+                o_g[:, u * HALF + n0 : u * HALF + n1, :].rearrange("p (a i) t -> p a t i", i=4),
+                res[u][:, :, n0:n1].rearrange("p t (a i) -> p a t i", i=4),
             )
 
         def planes(u):
@@ -190,48 +192,48 @@ def tile_picked_zshift_gelu_po_kernel(
                 out=o_w[:, tok].bitcast(FP8X4), scales=o_s[:, tok], in_=o_g[:, tok, :].rearrange("p n t -> p (n t)")
             )
 
-        for moving_w, moving_s, count in ((xq_w, xq_s, WARM_EARLY), (xp_w, xp_s, WARM_LATE)):
-            for t in range(count):
-                cols = slice(t * P, (t + 1) * P)
-                mm(gate_bank[3][:], xq_w[:, cols], xq_s[:, cols], moving_w[:], moving_s[:], True, True)
-        cast(nc.scalar.copy, w3_g, w3_raw, 0, HALF)
-        cast(nc.scalar.copy, w3_g, w3_raw, HALF, H)
-        w3q = quantize("w3q", w3_g)
-        cast(nc.scalar.copy, w4_g, w4_raw, 0, HALF)
-        cast(nc.scalar.copy, w4_g, w4_raw, HALF, W4_SCALAR)
-        cast(nc.vector.tensor_copy, w4_g, w4_raw, W4_SCALAR, H)
-        w4q = quantize("w4q", w4_g)
+        for t in range(WARM):
+            cols = slice(t * P, (t + 1) * P)
+            mm(warm_bank[:], xq_w[:, cols], xq_s[:, cols], xq_w[:], xq_s[:], True, True)
+        w3q = (tile("w3q_w", [P, H], I32), tile("w3q_s", [P, H], U8))
+        w4q = (tile("w4q_w", [P, H], I32), tile("w4q_s", [P, H], U8))
+        cast(nc.scalar.copy, w3_g, w3_raw, 0, 0)
+        cast(nc.scalar.copy, w3_g, w3_raw, 1, 0)
+        quantize(*w3q, w3_g[:, 0:2], 0)
+        quantize(*w3q, w3_g[:, 2:PACK], 2)
+        cast(nc.scalar.copy, w4_g[0], w4_raw, 0, 0)
+        cast(nc.scalar.copy, w4_g[1], w4_raw, 0, 2)
+        cast(nc.vector.tensor_copy, w4_g[0], w4_raw, 1, 0)
+        cast(nc.scalar.copy, w4_g[1], w4_raw, 1, 2, 0, LAST_SCALAR)
+        cast(nc.vector.tensor_copy, w4_g[1], w4_raw, 1, 2, LAST_SCALAR)
+        quantize(*w4q, w4_g[0][:], 0)
+        quantize(*w4q, w4_g[1][:], 2)
         w1d = deal_words("w1d", w1_raw, "w4_raw1")
         w2d = deal_words("w2d", w2_raw)
         ws = deal_scales("ws", ws_raw)
         w5d = deal_words("w5d", w5_raw)
-        h_half = tile("h_half", [P, S, PACK], BF16, "ws_raw")
         for c in range(CHUNKS):
             passes(by_chunk(hy_bank[c]), 0, w3q[0], w3q[1], xq_w, xq_s, tokens(c), True, False)
-        for c in range(CHUNKS - 1):
+        for c in range(CHUNKS):
             hidden(c)
-        gate_products(0)
-        for c in range(CHUNKS - 1):
+        for c in range(CHUNKS):
             halve(c)
             hidden_codes(c)
-        hidden(CHUNKS - 1)
-        halve(CHUNKS - 1)
-        hidden_codes(CHUNKS - 1)
-        second(0)
+        gate_products(0)
         gate_products(1)
-        second(1)
         gate_products(2)
+        second(0)
+        second(1)
         gate_products(3)
         second(2)
         second(3)
         for b in range(4):
             gated(b)
         o_g = tile("o_g", [P, S, PACK], BF16, "w2d")
-        round_out(0, nc.scalar.copy)
-        round_out(1, nc.scalar.copy)
+        round_out(nc.scalar.copy, 0, 0, HALF)
         o_s = tile("o_s", [P, S], U8, "gate3")
-        round_out(2, nc.vector.tensor_copy)
-        round_out(3, nc.scalar.copy)
+        round_out(nc.vector.tensor_copy, 1, 0, ROUND_VECTOR)
+        round_out(nc.scalar.copy, 1, ROUND_VECTOR, HALF)
         planes(0)
         nc.sync.dma_start(words_view(out_1)[:, 0:HALF], o_w[:, 0:HALF])
         planes(1)

@@ -45,7 +45,7 @@ def tile_picked_zshift_gelu_po_kernel(
         xw = tile("xw", [P, T], I32)
         xs = tile("xs", [P, T], U8)
         ws_stage = tile("ws_stage", [P, N], U8)
-        ws_raw = tile("ws_raw", [P, N], U8)
+        ws = tile("ws", [P, N], U8)
         w1_raw = tile("w1_raw", [P, N], I32)
         w2_raw = tile("w2_raw", [P, N], I32)
         w5_raw = tile("w5_raw", [P, N], I32)
@@ -76,8 +76,6 @@ def tile_picked_zshift_gelu_po_kernel(
             load_half(w4_raw, w4, u)
         nc.sync.dma_start(w1_raw[:], words_view(w1_words))
         nc.sync.dma_start(w2_raw[:], words_view(w2_words))
-        for q in range(4):
-            nc.sync.dma_start(ws_raw[32 * q : 32 * q + 32, :].bitcast(I32), ws_stage[q:P:4, :].bitcast(I32))
         nc.sync.dma_start(w5_raw[:], words_view(w5_words))
 
         xq_w = tile("xq_w", [P, S], I32)
@@ -153,7 +151,7 @@ def tile_picked_zshift_gelu_po_kernel(
             nc.scalar.activation(h_g[c][:], hy_bank[c][:].rearrange("p (t n) -> p n t", t=PACK), ACT.Gelu_apprx_tanh)
 
         def halve(c):
-            h_half[c] = tile(f"h_half{c}", [P, CHUNK, PACK], BF16, ("ws_raw", "w5_raw")[c % 2])
+            h_half[c] = tile(f"h_half{c}", [P, CHUNK, PACK], BF16, f"h_half{c % 2}")
             nc.vector.tensor_scalar(h_half[c][:], h_g[c][:], 0.5, None, ALU.mult)
 
         def hidden_codes(c):
@@ -195,6 +193,9 @@ def tile_picked_zshift_gelu_po_kernel(
         for t in range(WARM):
             cols = slice(t * P, (t + 1) * P)
             mm(warm_bank[:], xq_w[:, cols], xq_s[:, cols], xq_w[:], xq_s[:], True, True)
+        ws_dealt = deal_scales("ws_dealt", ws_stage)
+        for q in range(4):
+            nc.sync.dma_start(ws[32 * q : 32 * q + 32, :].bitcast(I32), ws_dealt[q:P:4, :].bitcast(I32))
         w3q = (tile("w3q_w", [P, H], I32), tile("w3q_s", [P, H], U8))
         w4q = (tile("w4q_w", [P, H], I32), tile("w4q_s", [P, H], U8))
         cast(nc.scalar.copy, w3_g, w3_raw, 0, 0)
@@ -210,7 +211,6 @@ def tile_picked_zshift_gelu_po_kernel(
         quantize(*w4q, w4_g[1][:], 2)
         w1d = deal_words("w1d", w1_raw, "w4_raw1")
         w2d = deal_words("w2d", w2_raw)
-        ws = deal_scales("ws", ws_raw)
         w5d = deal_words("w5d", w5_raw)
         for c in range(CHUNKS):
             passes(by_chunk(hy_bank[c]), 0, w3q[0], w3q[1], xq_w, xq_s, tokens(c), True, False)

@@ -21,7 +21,6 @@ CHUNK = 128
 HALF = 256
 CHUNKS = S // CHUNK
 ROUND_VECTOR = 160
-LAST_SCALAR = 40
 WARM = 4
 
 
@@ -103,11 +102,10 @@ def tile_picked_zshift_gelu_po_kernel(
             )
             return dealt
 
-        def cast(copy, grouped, raw, u, t0, m0=0, m1=HALF // PACK):
-            first = u * HALF // PACK
+        def cast(copy, grouped, raw, u, t0):
             copy(
-                grouped[:, :, first + m0 : first + m1, :].rearrange("p t m j -> p m j t"),
-                raw[u][:].rearrange("p j (m t) -> p m j t", t=PACK)[:, m0:m1, :, t0 : t0 + grouped.shape[1]],
+                grouped[:, :, u * HALF // PACK : (u + 1) * HALF // PACK, :].rearrange("p t m j -> p m j t"),
+                raw[u][:].rearrange("p j (m t) -> p m j t", t=PACK)[:, :, :, t0 : t0 + grouped.shape[1]],
             )
 
         def quantize(codes, plane, grouped, t0):
@@ -125,9 +123,6 @@ def tile_picked_zshift_gelu_po_kernel(
                 cols = slice((first + e) * P, (first + e + 1) * P)
                 mm(out, words[:, cols], plane[:, cols], x_w[:, tok], x_s[:, tok], opens and e == 0, closes and e == len(outs) - 1)
 
-        def by_chunk(bank):
-            return [bank[:, t * CHUNK : (t + 1) * CHUNK] for t in range(PACK)]
-
         def by_half(bank):
             return [bank[:, e * HALF : (e + 1) * HALF] for e in range(2)]
 
@@ -140,22 +135,23 @@ def tile_picked_zshift_gelu_po_kernel(
         warm_bank = psum.tile([P, S], F32, name="warm_bank")
         gate_bank = {}
         gate = [tile(f"gate{b}", [P, S], F32) for b in range(4)]
-        h_g = {}
+        h_g = [tile(f"h_g{u}", [P, 2, HALF, 2], BF16) for u in range(2)]
         h_half = {}
         h_w = tile("h_w", [P, S], I32)
         h_s = tile("h_s", [P, S], U8)
 
-        def hidden(c):
-            passes(by_chunk(hy_bank[c]), 0, w4q[0], w4q[1], xp_w, xp_s, tokens(c), False, True)
-            h_g[c] = tile(f"h_g{c}", [P, CHUNK, PACK], BF16, f"h_g{c}")
-            nc.scalar.activation(h_g[c][:], hy_bank[c][:].rearrange("p (t n) -> p n t", t=PACK), ACT.Gelu_apprx_tanh)
+        def hidden(b):
+            u, pair = divmod(b, 2)
+            passes(by_half(hy_bank[b]), 2 * pair, w4q[0], w4q[1], xp_w, xp_s, half_tokens(u), False, True)
+            nc.scalar.activation(h_g[u][:, pair], hy_bank[b][:].rearrange("p (e n) -> p n e", e=2), ACT.Gelu_apprx_tanh)
 
         def halve(c):
-            h_half[c] = tile(f"h_half{c}", [P, CHUNK, PACK], BF16, f"h_half{c % 2}")
-            nc.vector.tensor_scalar(h_half[c][:], h_g[c][:], 0.5, None, ALU.mult)
+            u, part = divmod(c, 2)
+            h_half[c] = tile(f"h_half{c}", [P, CHUNK, 2, 2], BF16, f"h_half{c % 2}")
+            nc.vector.tensor_scalar(h_half[c][:], h_g[u][:, :, tokens(part), :].rearrange("p r n e -> p n r e"), 0.5, None, ALU.mult)
 
         def hidden_codes(c):
-            nc.vector.quantize_mx(out=h_w[:, tokens(c)].bitcast(FP8X4), scales=h_s[:, tokens(c)], in_=h_half[c][:].rearrange("p n t -> p (n t)"))
+            nc.vector.quantize_mx(out=h_w[:, tokens(c)].bitcast(FP8X4), scales=h_s[:, tokens(c)], in_=h_half[c][:].rearrange("p n r e -> p (n r e)"))
 
         def gate_products(b):
             u, pair = divmod(b, 2)
@@ -205,20 +201,21 @@ def tile_picked_zshift_gelu_po_kernel(
         cast(nc.scalar.copy, w4_g[0], w4_raw, 0, 0)
         cast(nc.scalar.copy, w4_g[1], w4_raw, 0, 2)
         cast(nc.vector.tensor_copy, w4_g[0], w4_raw, 1, 0)
-        cast(nc.scalar.copy, w4_g[1], w4_raw, 1, 2, 0, LAST_SCALAR)
-        cast(nc.vector.tensor_copy, w4_g[1], w4_raw, 1, 2, LAST_SCALAR)
+        cast(nc.scalar.copy, w4_g[1], w4_raw, 1, 2)
         quantize(*w4q, w4_g[0][:], 0)
         quantize(*w4q, w4_g[1][:], 2)
         w1d = deal_words("w1d", w1_raw, "w4_raw1")
         w2d = deal_words("w2d", w2_raw)
         w5d = deal_words("w5d", w5_raw)
-        for c in range(CHUNKS):
-            passes(by_chunk(hy_bank[c]), 0, w3q[0], w3q[1], xq_w, xq_s, tokens(c), True, False)
-        for c in range(CHUNKS):
-            hidden(c)
-        for c in range(CHUNKS):
-            halve(c)
-            hidden_codes(c)
+        for b in range(4):
+            u, pair = divmod(b, 2)
+            passes(by_half(hy_bank[b]), 2 * pair, w3q[0], w3q[1], xq_w, xq_s, half_tokens(u), True, False)
+        for b in range(4):
+            hidden(b)
+        for u in range(2):
+            for step in (halve, hidden_codes):
+                for part in range(2):
+                    step(2 * u + part)
         gate_products(0)
         gate_products(1)
         gate_products(2)

from contextlib import ExitStack

import concourse.mybir as mybir

K, T, S, H, N = 512, 1024, 512, 512, 512
FLOPS = 5 * 2 * 512 * 512 * 512

F32 = mybir.dt.float32
BF16 = mybir.dt.bfloat16
I32 = mybir.dt.int32
U32 = mybir.dt.uint32
U16 = mybir.dt.uint16
U8 = mybir.dt.uint8
FP8X4 = mybir.dt.float8_e4m3fn_x4
ACT = mybir.ActivationFunctionType
ALU = mybir.AluOpType

P = 128
PACK = 4
CHUNK = 128
HALF = 256
CHUNKS = S // CHUNK
ROUND_VECTOR = 160
WARM = 4


def tile_picked_zshift_gelu_po_kernel(
    tc, x_words, x_scales, w1_words, w1_scales, w2_words, w2_scales, w3, w4, w5_words, w5_scales, offs, prev,
    out_0, out_1, out_2,
):
    nc = tc.nc
    with ExitStack() as ctx:
        sb = ctx.enter_context(tc.tile_pool(name="sb", bufs=1))
        psum = ctx.enter_context(tc.psum_pool(name="psum", bufs=1))

        def tile(name, shape, dtype, tag=None):
            return sb.tile(shape, dtype, name=name, tag=tag or name, align_bytes=64)

        def words_view(dram):
            return dram[0].rearrange("p n t -> p (n t)").bitcast(I32)

        offs_sb = sb.tile([P, S // 16], U16, name="offs_sb")
        prev_sb = sb.tile([P, S // 16], U16, name="prev_sb")
        xw = tile("xw", [P, T], I32)
        xs = tile("xs", [P, T], U8)
        ws_stage = tile("ws_stage", [P, N], U8)
        ws = tile("ws", [P, N], U8)
        w1_raw = tile("w1_raw", [P, N], I32)
        w2_raw = tile("w2_raw", [P, N], I32)
        w5_raw = tile("w5_raw", [P, N], I32)
        w3_raw = [tile(f"w3_raw{u}", [P, PACK, HALF], F32) for u in range(2)]
        w4_raw = [tile(f"w4_raw{u}", [P, PACK, HALF], F32) for u in range(2)]
        warm = tile("warm", [P, 2], F32)

        def load_x_scales(queue, q):
            rows = x_scales[0].bitcast(I32)[4 * q : 4 * q + 4, :]
            queue.dma_start(xs[32 * q : 32 * q + 32, :].bitcast(I32), rows.partition_broadcast(8))

        def load_half(raw, dram, u):
            nc.sync.dma_start(raw[u][:], dram.rearrange("(p j) c -> p j c", j=PACK)[:, :, u * HALF : (u + 1) * HALF])

        nc.vector.memset(warm[:, 0:1], 0.0)
        nc.vector.memset(ws_stage[:].bitcast(I32), 0)
        nc.sync.dma_start(offs_sb[:], offs)
        for q in range(4):
            load_x_scales(nc.scalar if q < 2 else nc.sync, q)
        nc.sync.dma_start(xw[:], words_view(x_words))
        nc.sync.dma_start(prev_sb[:], prev)
        nc.scalar.activation(warm[:, 1:2], warm[:, 0:1], ACT.Gelu_apprx_tanh)
        load_half(w3_raw, w3, 0)
        for w, dram in enumerate((w1_scales, w2_scales, w5_scales)):
            nc.sync.dma_start(ws_stage[16 * w : 16 * w + 16, :].bitcast(I32), dram[0].bitcast(I32).rearrange("(q r) c -> r q c", r=4))
        load_half(w3_raw, w3, 1)
        for u in range(2):
            load_half(w4_raw, w4, u)
        nc.sync.dma_start(w1_raw[:], words_view(w1_words))
        nc.sync.dma_start(w2_raw[:], words_view(w2_words))
        nc.sync.dma_start(w5_raw[:], words_view(w5_words))

        xq_w = tile("xq_w", [P, S], I32)
        xp_w = tile("xp_w", [P, S], I32)
        xq_s = tile("xq_s", [P, S], U8)
        xp_s = tile("xp_s", [P, S], U8)
        nc.vector.tensor_copy(xq_s[:], xs[:].indirect(offs_sb[:]))
        nc.vector.tensor_copy(xq_w[:].bitcast(U32), xw[:].bitcast(U32).indirect(offs_sb[:]))
        nc.vector.tensor_copy(xp_s[:], xs[:].indirect(prev_sb[:]))
        nc.vector.tensor_copy(xp_w[:].bitcast(U32), xw[:].bitcast(U32).indirect(prev_sb[:]))

        def deal_words(name, raw, tag=None):
            dealt = tile(name, [P, N], I32, tag)
            nc.vector.tensor_copy(
                dealt[:].rearrange("p (t c i) -> p c t i", t=PACK, i=4),
                raw[:].rearrange("p (c i t) -> p c t i", t=PACK, i=4),
            )
            return dealt

        def deal_scales(name, raw, tag=None):
            dealt = tile(name, [P, N], U8, tag)
            nc.vector.tensor_copy(
                dealt[:].rearrange("p (t c i) -> p c t i", t=PACK, i=16),
                raw[:].rearrange("p (c i t) -> p c t i", t=PACK, i=16),
            )
            return dealt

        def cast(copy, grouped, raw, u, t0):
            copy(
                grouped[:, :, u * HALF // PACK : (u + 1) * HALF // PACK, :].rearrange("p t m j -> p m j t"),
                raw[u][:].rearrange("p j (m t) -> p m j t", t=PACK)[:, :, :, t0 : t0 + grouped.shape[1]],
            )

        def quantize(codes, plane, grouped, t0):
            cols = slice(t0 * P, (t0 + grouped.shape[1]) * P)
            nc.vector.quantize_mx(out=codes[:, cols].bitcast(FP8X4), scales=plane[:, cols], in_=grouped.rearrange("p t m j -> p (t m j)"))

        def mm(out, lw, ls, rw, rs, start, stop):
            nc.tensor.matmul_mx(out=out, lhsT=lw.bitcast(FP8X4), lhsT_scale=ls, rhs=rw.bitcast(FP8X4), rhs_scale=rs, start=start, stop=stop)

        def tokens(c):
            return slice(c * CHUNK, (c + 1) * CHUNK)

        def passes(outs, first, words, plane, x_w, x_s, tok, opens, closes):
            for e, out in enumerate(outs):
                cols = slice((first + e) * P, (first + e + 1) * P)
                mm(out, words[:, cols], plane[:, cols], x_w[:, tok], x_s[:, tok], opens and e == 0, closes and e == len(outs) - 1)

        def by_half(bank):
            return [bank[:, e * HALF : (e + 1) * HALF] for e in range(2)]

        def half_tokens(u):
            return slice(u * HALF, (u + 1) * HALF)

        w3_g = tile("w3_g", [P, PACK, P, PACK], BF16)
        w4_g = [tile(f"w4_g{pair}", [P, 2, P, PACK], BF16) for pair in range(2)]
        hy_bank = [psum.tile([P, S], F32, name=f"hy_bank{b}") for b in range(4)]
        warm_bank = psum.tile([P, S], F32, name="warm_bank")
        gate_bank = {}
        gate = [tile(f"gate{b}", [P, S], F32) for b in range(4)]
        h_g = [tile(f"h_g{u}", [P, 2, HALF, 2], BF16) for u in range(2)]
        h_half = {}
        h_w = tile("h_w", [P, S], I32)
        h_s = tile("h_s", [P, S], U8)

        def hidden(b):
            u, pair = divmod(b, 2)
            passes(by_half(hy_bank[b]), 2 * pair, w4q[0], w4q[1], xp_w, xp_s, half_tokens(u), False, True)
            nc.scalar.activation(h_g[u][:, pair], hy_bank[b][:].rearrange("p (e n) -> p n e", e=2), ACT.Gelu_apprx_tanh)

        def halve(c):
            u, part = divmod(c, 2)
            h_half[c] = tile(f"h_half{c}", [P, CHUNK, 2, 2], BF16, f"h_half{c % 2}")
            nc.vector.tensor_scalar(h_half[c][:], h_g[u][:, :, tokens(part), :].rearrange("p r n e -> p n r e"), 0.5, None, ALU.mult)

        def hidden_codes(c):
            nc.vector.quantize_mx(out=h_w[:, tokens(c)].bitcast(FP8X4), scales=h_s[:, tokens(c)], in_=h_half[c][:].rearrange("p n r e -> p (n r e)"))

        def gate_products(b):
            u, pair = divmod(b, 2)
            gate_bank[b] = psum.tile([P, S], F32, name=f"gate_bank{b}", tag=f"gate_bank{b % 3}")
            passes(by_half(gate_bank[b]), 2 * pair, w1d, ws, xq_w, xq_s, half_tokens(u), True, False)
            passes(by_half(gate_bank[b]), 2 * pair, w2d, ws[4:], xp_w, xp_s, half_tokens(u), False, True)
            nc.scalar.activation(gate[b][:], gate_bank[b][:], ACT.Tanh, scale=0.5)

        def second(b):
            u, pair = divmod(b, 2)
            passes(by_half(hy_bank[b]), 2 * pair, w5d, ws[8:], h_w, h_s, half_tokens(u), True, True)

        out_rows = out_0.rearrange("(p t) n -> p t n", t=PACK)
        o_w = tile("o_w", [P, S], I32)
        res = [tile(f"res{u}", [P, PACK, HALF], F32) for u in range(2)]

        def gated(b):
            u, pair = divmod(b, 2)
            piece = res[u][:, 2 * pair : 2 * pair + 2, :]
            nc.vector.scalar_tensor_tensor(piece.rearrange("p t n -> p (t n)"), gate[b][:], 1.0, hy_bank[b][:], ALU.add, ALU.mult)
            nc.sync.dma_start(out_rows[:, 2 * pair : 2 * pair + 2, half_tokens(u)], piece)

        def round_out(copy, u, n0, n1):
            copy(
                o_g[:, u * HALF + n0 : u * HALF + n1, :].rearrange("p (a i) t -> p a t i", i=4),
                res[u][:, :, n0:n1].rearrange("p t (a i) -> p a t i", i=4),
            )

        def planes(u):
            tok = half_tokens(u)
            nc.vector.quantize_mx(
                out=o_w[:, tok].bitcast(FP8X4), scales=o_s[:, tok], in_=o_g[:, tok, :].rearrange("p n t -> p (n t)")
            )

        for t in range(WARM):
            cols = slice(t * P, (t + 1) * P)
            mm(warm_bank[:], xq_w[:, cols], xq_s[:, cols], xq_w[:], xq_s[:], True, True)
        ws_dealt = deal_scales("ws_dealt", ws_stage)
        for q in range(4):
            nc.sync.dma_start(ws[32 * q : 32 * q + 32, :].bitcast(I32), ws_dealt[q:P:4, :].bitcast(I32))
        w3q = (tile("w3q_w", [P, H], I32), tile("w3q_s", [P, H], U8))
        w4q = (tile("w4q_w", [P, H], I32), tile("w4q_s", [P, H], U8))
        cast(nc.scalar.copy, w3_g, w3_raw, 0, 0)
        cast(nc.scalar.copy, w3_g, w3_raw, 1, 0)
        quantize(*w3q, w3_g[:, 0:2], 0)
        quantize(*w3q, w3_g[:, 2:PACK], 2)
        cast(nc.scalar.copy, w4_g[0], w4_raw, 0, 0)
        cast(nc.scalar.copy, w4_g[1], w4_raw, 0, 2)
        cast(nc.vector.tensor_copy, w4_g[0], w4_raw, 1, 0)
        cast(nc.scalar.copy, w4_g[1], w4_raw, 1, 2)
        quantize(*w4q, w4_g[0][:], 0)
        quantize(*w4q, w4_g[1][:], 2)
        w1d = deal_words("w1d", w1_raw, "w4_raw1")
        w2d = deal_words("w2d", w2_raw)
        w5d = deal_words("w5d", w5_raw)
        for b in range(4):
            u, pair = divmod(b, 2)
            passes(by_half(hy_bank[b]), 2 * pair, w3q[0], w3q[1], xq_w, xq_s, half_tokens(u), True, False)
        for b in range(4):
            hidden(b)
        for u in range(2):
            for step in (halve, hidden_codes):
                for part in range(2):
                    step(2 * u + part)
        gate_products(0)
        gate_products(1)
        gate_products(2)
        second(0)
        second(1)
        gate_products(3)
        second(2)
        second(3)
        for b in range(4):
            gated(b)
        o_g = tile("o_g", [P, S, PACK], BF16, "w2d")
        round_out(nc.scalar.copy, 0, 0, HALF)
        o_s = tile("o_s", [P, S], U8, "gate3")
        round_out(nc.vector.tensor_copy, 1, 0, ROUND_VECTOR)
        round_out(nc.scalar.copy, 1, ROUND_VECTOR, HALF)
        planes(0)
        nc.sync.dma_start(words_view(out_1)[:, 0:HALF], o_w[:, 0:HALF])
        planes(1)
        nc.scalar.dma_start(words_view(out_1)[:, HALF:S], o_w[:, HALF:S])
        scale_rows = out_2[0].bitcast(I32)
        for q in range(4):
            queue = nc.scalar if q % 2 == 0 else nc.sync
            queue.dma_start(scale_rows[4 * q : 4 * q + 4, :], o_s[32 * q : 32 * q + 4, :].bitcast(I32))
